import numpy as np, ml_dtypes
CORES = [2,3,42,43,82,83,122,123]
N = 8
BF = ml_dtypes.bfloat16
def gentries(a):
    return np.ascontiguousarray(a.reshape(8, 16, -1).transpose(0, 2, 1)).reshape(8, -1)
def gtable(e):
    e = np.asarray(e); return np.ascontiguousarray(e.reshape(8, -1, 16).transpose(0, 2, 1)).reshape(128, -1).astype(np.int32)
I, V, G, M, RO = 1024, 353, 96, 1024, 3
def grow(J):
    T = J.shape[0]; ar = np.arange(T); ch = np.zeros((T, 2 * I), np.int64); free = np.zeros((T, I + 1), np.int64); free[:, 1] = 1
    for t in range(1, I):
        j = J[:, t]; ch[ar, free[ar, j]] = t; free[ar, j] = 2 * t; free[:, t + 1] = 2 * t + 1
    ch[ar[:, None], free] = I + np.arange(I + 1)[None, :]
    return ch.reshape(T, I, 2)
def trees(rng, kind, lab):
    T = N * 8; k = kind.reshape(T, 1); t = np.arange(I)[None, :]; r = rng.random((T, I))
    level = t + 1 - 2 ** (np.frexp((t + 1).astype(np.float64))[1].astype(np.int64) - 1)
    J = np.where(k == 0, (r * (t + 1)).astype(np.int64), np.where(k == 1, t - np.minimum((4 * r).astype(np.int64), t), np.where(k == 2, t, level)))
    ch = grow(J); b = lab.reshape(T, 1); s = np.arange(I + 1)[None, :]
    pi = np.where(b == 0, np.argsort(rng.random((T, I)), axis=1), np.where(b == 1, t, I - 1 - t))
    lf = I + np.where(b == 0, np.argsort(rng.random((T, I + 1)), axis=1), np.where(b == 1, s, I - s))
    c = np.take_along_axis(np.concatenate([pi, lf], axis=1), ch.reshape(T, 2 * I), 1).reshape(T, I, 2)
    c = np.where(rng.random((T, I, 1)) < 0.5, c[:, :, ::-1], c)
    o = np.zeros_like(c); o[np.arange(T)[:, None], pi] = c
    return o[:, :, 0].reshape(N, 8, I), o[:, :, 1].reshape(N, 8, I)
def parts(rng):
    size = rng.random((N, 8, 1, I + V)); size[..., :I] = 0.4 + 0.6 * size[..., :I]
    h = np.minimum((256 * size * rng.random((N, 8, 16, I + V))).astype(np.int64), 255)
    return h, rng.integers(-50, 51, (N, 8, 16, V)), rng.integers(0, V, (N, 8, N - 1, G))
def pack(h, v, tr, s):
    return {"h0": np.ascontiguousarray(h.reshape(N, 128, I + V)).astype(np.int32), "vel": np.ascontiguousarray(v.reshape(N, 128, V)).astype(np.int32),
            "kl": np.stack([gtable(a) for a in tr[0]]), "kr": np.stack([gtable(a) for a in tr[1]]), "sl": np.stack([gtable(a.reshape(8, -1)) for a in s])}
def setup_inputs(rng):
    h, v, s = parts(rng)
    return pack(h, v, trees(rng, rng.integers(0, 2, (N, 8)), np.zeros((N, 8), np.int64)), s)
def setup_inputs_ties(rng):
    h, v, s = parts(rng)
    h[:, ::2] = 8 * rng.integers(0, 4, (N, 4, 1, I + V)); h[:, ::2, :, :I] += 16
    v[:, ::2] = 8 * rng.integers(-1, 2, (N, 4, 1, V))
    h[:, 1::2] = 100 + (rng.random((N, 4, 16, I + V)) < 0.0625); v[:, 1::2] = rng.integers(-1, 2, (N, 4, 1, V))
    return pack(h, v, trees(rng, rng.integers(0, 4, (N, 8)), rng.integers(0, 3, (N, 8))), s)
def setup_inputs_chain(rng):
    h, v, s = parts(rng)
    kind = np.tile(np.array([2, 3, 2, 1, 2, 3, 2, 0]), (N, 1)); lab = rng.integers(0, 3, (N, 8)); lab[:, 0] = np.arange(N) % 3; lab[:, 4] = (np.arange(N) + 1) % 3
    for g in (0, 4): h[:, g, :, :I] = 255; h[:, g, :, I:] = 0
    lab[:, 2] = 1 + np.arange(N) % 2; node = np.arange(I)[None, :]
    depth = np.where(lab[:, 2:3] == 1, node, I - 1 - node)
    h[:, 2, :, :I] = rng.integers(0, 128, (N, 16, I)) + 128 * (depth % 2)[:, None, :]; h[:, 2, :, I:] = 0
    return pack(h, v, trees(rng, kind, lab), s)
def setup_inputs_edge(rng):
    h, v, s = parts(rng)
    h = 255 * (rng.random(h.shape) < rng.random((N, 8, 1, I + V))).astype(np.int64); h[:, 3, :, :I] = 255; h[:, 3, :, I:] = 0
    v = 127 * rng.integers(-1, 2, v.shape); s[:, ::2] = (V - 1) * rng.integers(0, 2, (N, 4, N - 1, G))
    lab = rng.integers(1, 3, (N, 8)); lab[:, 0] = 1; lab[:, 1] = 2
    tr = trees(rng, rng.integers(0, 4, (N, 8)), lab)
    c = np.stack([tr[0][0, 0], tr[1][0, 0]], axis=1)
    w = int(c[0][c[0] != 1][0]); low = np.concatenate([np.array([w]), c[1], c[w:w + 1].reshape(-1)]); low = low[low < I + V]
    h[0, 0][:, low] = 0; h[0, 0][:, 1] = 255
    return pack(h, v, tr, s)
def setup_inputs_alike(rng):
    h, v, s = parts(rng); kl, kr = trees(rng, np.zeros((N, 8), np.int64), np.zeros((N, 8), np.int64))
    kl[:] = kl[:, :1]; kr[:] = kr[:, :1]
    g = rng.permutation(8); h[:, g[0], :, :I] = 0; h[:, g[1:3]] = h[:, g[1:3], :1]
    s = rng.choice(np.array([0, V - 1, V // 2, 3]), s.shape)
    return pack(h, v, (kl, kr), s)
def setup_inputs_spread(rng):
    h, v, s = parts(rng)
    h = np.minimum((np.exp2(1 + 8 * rng.random((N, 8, 1, I + V))) * rng.random(h.shape)).astype(np.int64), 255)
    v = np.minimum((np.exp2(7 * rng.random((N, 8, 1, V))) * rng.random(v.shape)).astype(np.int64), 127) * (2 * rng.integers(0, 2, v.shape) - 1)
    return pack(h, v, trees(rng, rng.integers(0, 4, (N, 8)), np.zeros((N, 8), np.int64)), s)
def check_inputs(d):
    bad = []
    for k, lo, hi in (("h0", 0, 255), ("vel", -127, 127), ("kl", 0, 2 * I), ("kr", 0, 2 * I), ("sl", 0, V - 1)):
        if np.min(d[k]) < lo or np.max(d[k]) > hi: bad.append("range of " + k)
    if bad: return bad
    for q in range(N):
        c = np.concatenate([gentries(d["kl"][q]), gentries(d["kr"][q])], axis=1).astype(np.int64); o = np.sort(c, axis=1)
        if np.any(o[:, 1:] == o[:, :-1]):
            bad.append("children all differ"); break
        up = np.tile(np.arange(2 * I + 1), (8, 1)); np.put_along_axis(up, c, np.tile(np.arange(I), (8, 2)), 1)
        for i in range(13): up = np.take_along_axis(up, up, 1)
        if np.any(up != up[:, :1]):
            bad.append("one tree"); break
    return bad
def reference(h0, vel, kl, kr, sl):
    E = 2 * I + 1; at = np.arange(I)
    H = np.zeros((N, 8, 16, E), np.int64); H[..., :I + V] = h0.reshape(N, 8, 16, I + V)
    v = vel.astype(np.int64).reshape(N, 8, 16, V); s = np.stack([gentries(a) for a in sl]).astype(np.int64).reshape(N, 8, N - 1, G)
    K = np.stack([np.stack([gentries(kl[q]), gentries(kr[q])], axis=1) for q in range(N)]).astype(np.int64)
    for rnd in range(RO):
        for q in range(N):
            for d in range(1, N):
                o = (q - d) % N; j = I + V + (d - 1) * G
                H[q, :, :, j:j + G] = np.take_along_axis(H[o, :, :, I:I + V], s[o, :, d - 1][:, None, :], 2)
        hc = [np.take_along_axis(H, K[:, :, a][:, :, None, :], 3) for a in (0, 1)]
        best = np.zeros((N, 8, I), np.int64); ca = np.zeros_like(best); cb = np.zeros_like(best)
        for a in (0, 1):
            inner = K[:, :, a] < I; u = np.where(inner, K[:, :, a], 0); su = np.add.reduce(hc[a], axis=2)
            for b in (0, 1):
                z = np.take_along_axis(K[:, :, 1 - b], u, 2)
                gain = su - np.add.reduce(np.maximum(hc[1 - a], np.take_along_axis(H, z[:, :, None, :], 3)), axis=2)
                more = inner & (gain > best); best = np.where(more, gain, best); ca = np.where(more, a, ca); cb = np.where(more, b, cb)
        key = np.full((N, 8, E + 1), -1, np.int64); key[..., :I] = np.where(best > 0, M * best + at, -1)
        par = np.full((N, 8, E), E, np.int64)
        for a in (0, 1): np.put_along_axis(par, K[:, :, a], np.tile(at, (N, 8, 1)), 2)
        near = np.take_along_axis(key, par[..., :I], 2)
        for a in (0, 1): near = np.maximum(near, np.take_along_axis(key, K[:, :, a], 2))
        q, g, n = np.nonzero(key[..., :I] > near); a = ca[q, g, n]; b = cb[q, g, n]
        u = K[q, g, a, n]; w = K[q, g, 1 - a, n]; x = K[q, g, b, u]
        K[q, g, 1 - a, n] = x; K[q, g, b, u] = w
        new = np.maximum(np.take_along_axis(H, K[:, :, 0][:, :, None, :], 3), np.take_along_axis(H, K[:, :, 1][:, :, None, :], 3))
        H[..., I:I + V] = np.minimum(np.maximum(H[..., I:I + V] + v, 0), 255); H[..., :I] = new
    return {"yh": H[..., :I + V].reshape(N, 128, I + V).astype(np.float32), "yk": K.reshape(N, 8, 2 * I).astype(np.float32)}

@@ -1,0 +1,482 @@
+from concourse.bass import DstId, RemoteDMATransfer
+from concourse.mybir import AluOpType, ActivationFunctionType
+
+OP = AluOpType
+AF = ActivationFunctionType
+I, V0, GH, RO = 1024, 353, 96, 3
+LEAF, WIN = 2120, 2113
+
+SCRATCH = {"b%d" % _b: ("psum", [128, 512], "float32") for _b in range(8)}
+for _dt, _names in (
+        ("int32", "hl 360 hi 1024 vi 360 si 48 pi 8 pq 8 KI 128 CI 256 PI 64 CIP 128 gi 64"),
+        ("uint16", "su 48 KU 128 KB 128 PB 64 PPu 64"),
+        ("bfloat16", "HA 2064 HB 2064 vo 368 sh 672 sv 672 lh 672 lv 672 hcl 2064 hcr 2064 hr2 1024 mm 3072 zz 1024 rl 1024 rr 1024 "
+                     "GW 2120 CW 2120 gl 1024 gr 1024 gp 1024 cp 1024 cg 1024 ones 144 ec 144 ES 2304 bc 16 BS 144 BSn 144 sG 144 sL 144 "
+                     "sR 144 sS 144 sC 144 sC2 144 sPn 144 sPB 144 sRC 144 id1 128 idn 128 idn16 128 id64 128 idk 128 CK 256 LF 128 "
+                     "TB 192 CKP 128 LFP 64 LF16 64 ghi 64 glo 64 code 64 fh 128 fl 128 nch 128 cq 256"),
+        ("float32", "y1 1032 PW 2056 nrow 1024 sC32 144 id32 128 qf 8 jr 16 oh 16 ww 16 c16 128 NN 128 inn 128 GPs 64 SUm 128 "
+                    "q1s 128 qq 128 ga 64 cd 64 cc 64 tt 192 rot 64 MK 256 pr 256 xs 128 K1 128 dS 128 sd 128 ee 128 te 128 "
+                    "pt 512 s4 64 OK 1024 OH 1384")):
+    _w = _names.split()
+    for _n, _c in zip(_w[::2], _w[1::2]):
+        SCRATCH[_n] = ("sbuf", [128, int(_c)], _dt)
+SEMAPHORES = ["V", "A", "P", "G", "arrH", "arrV", "sent"] + ["d%d" % _i for _i in range(16)]
+
+
+def sends(T, topo, q):
+    src = T.cores[q]
+    dst = {d: T.cores[(q + d) % 8] for d in range(1, 8)}
+    near = [d for d in dst if topo.chip(dst[d]) == topo.chip(src)]
+    far = [d for d in dst if d not in near]
+    pool = list(topo.engines(src, dst[far[0]]))
+
+    def direct(d):
+        a, b = topo.chip(src), topo.chip(dst[d])
+        return topo.mates(a, b) or topo.same_plane(a, b)
+    far.sort(key=lambda d: (direct(d), d))
+    out = {}
+    spare = len(pool) - len(far)
+    used = 0
+    for d in far:
+        k = 2 if spare > 0 else 1
+        spare -= k - 1
+        out[d] = pool[used:used + k]
+        used += k
+    rest = [e for e in topo.engines(src, dst[near[0]]) if e not in pool]
+    for j, d in enumerate(near):
+        out[d] = rest[j:j + 1]
+    return out
+
+
+def rank_program(g, core, T, topo):
+    rank = T.rank_of(core)
+    if rank is None:
+        return
+    queue = {"V": g.vector, "A": g.scalar, "P": g.tensor, "G": g, "S": g.sync}
+    cnt = {}
+    known = {q: {} for q in queue}
+    acc = {}
+    ndma = [0]
+
+    def psum(name):
+        return name[0] == "b" and name[1:].isdigit()
+
+    def hazards(q, rd, wr):
+        deps = []
+        for ops, w in ((rd, False), (wr, True)):
+            for _, name, a, b in ops:
+                if psum(name):
+                    deps += [r for qq, r in acc.setdefault(name, {}).items() if qq != q]
+                    continue
+                for k, x, y, r in acc.setdefault(name, []):
+                    if x < b and y > a and (w or k) and not (r[2] == q and (q == "P" or not k)):
+                        deps.append(r)
+        return deps
+
+    def note(q, rd, wr, rec):
+        for ops, w in ((rd, False), (wr, True)):
+            for _, name, a, b in ops:
+                if psum(name):
+                    acc[name][q] = rec
+                    continue
+                lst = acc[name]
+                if w:
+                    lst[:] = [t for t in lst if not (t[1] >= a and t[2] <= b)]
+                else:
+                    lst[:] = [t for t in lst if t[0] or t[3][2] != rec[2] or not (t[1] >= a and t[2] <= b)]
+                lst.append((w, a, b, rec))
+
+    def sync(q, deps):
+        kn = known[q]
+        best = {}
+        for r in deps:
+            if kn.get(r[0], 0) < r[1] and (r[0] not in best or best[r[0]][1] < r[1]):
+                best[r[0]] = r
+        for r in sorted(best.values(), key=lambda r: -len(r[3])):
+            if kn.get(r[0], 0) >= r[1]:
+                continue
+            queue[q].wait_ge(T.sem[r[0]], r[1])
+            for s, c in r[3].items():
+                kn[s] = max(kn.get(s, 0), c)
+            kn[r[0]] = r[1]
+
+    def emit(q, fns, rd, wr):
+        sync(q, hazards(q, rd, wr))
+        for f in fns:
+            f().then_inc(T.sem[q], 1)
+            cnt[q] = cnt.get(q, 0) + 1
+        note(q, rd, wr, (q, cnt[q], q, dict(known[q])))
+
+    def dma(q, out, in_, rd, wr):
+        sync(q, hazards(q, rd, wr))
+        s = "d%d" % ndma[0]
+        ndma[0] += 1
+        cnt[s] = 16
+        queue[q].dma_start(out, in_).then_inc(T.sem[s], 16)
+        note("D", rd, wr, (s, 16, "D", dict(known[q])))
+
+    def X(name, a, b, step=1):
+        return (T[name][:, a:b] if step == 1 else T[name][:, a:b:step], name, a, b)
+
+    def ind(win, off):
+        return (win[0].indirect(off[0]), win, off)
+
+    def flat(*ops):
+        out = []
+        for o in ops:
+            out += [o[1], o[2]] if len(o) == 3 else [o]
+        return out
+
+    def vcopy(out, in_):
+        if len(out) == 3:
+            emit("V", [lambda: g.vector.tensor_copy(out[0], in_[0])], [in_, out[2]], [out[1]])
+        else:
+            emit("V", [lambda: g.vector.tensor_copy(out[0], in_[0])], flat(in_), [out])
+
+    def vtt(out, a, b, op):
+        emit("V", [lambda: g.vector.tensor_tensor(out[0], a[0], b[0], op)], flat(a, b), [out])
+
+    def vts(out, a, s1, op0, s2=None, op1=None):
+        rd = [a] + [s for s in (s1, s2) if isinstance(s, tuple)]
+        v1 = s1[0] if isinstance(s1, tuple) else s1
+        v2 = s2[0] if isinstance(s2, tuple) else s2
+        if op1 is None:
+            emit("V", [lambda: g.vector.tensor_scalar(out[0], a[0], v1, None, op0)], rd, [out])
+        else:
+            emit("V", [lambda: g.vector.tensor_scalar(out[0], a[0], v1, v2, op0, op1)], rd, [out])
+
+    def vset(out, c):
+        emit("V", [lambda: g.vector.memset(out[0], c)], [], [out])
+
+    def act(out, in_, func=AF.Copy, scale=None, bias=None):
+        kw = {}
+        rd = flat(in_)
+        for key, v in (("scale", scale), ("bias", bias)):
+            if v is not None:
+                kw[key] = v[0] if isinstance(v, tuple) else v
+                rd = rd + ([v] if isinstance(v, tuple) else [])
+        emit("A", [lambda: g.scalar.activation(out[0], in_[0], func, **kw)], rd, [out])
+
+    def gsel(out, in_, pattern, op, base, cm):
+        emit("G", [lambda: g.affine_select(out[0], in_[0], pattern, op, 0.0, base, cm)], [in_], [out])
+
+    def giota(out, pattern, base, cm, flag):
+        kw = {"allow_small_or_imprecise_dtypes": True} if flag else {}
+        emit("G", [lambda: g.iota(out[0], pattern, base, cm, **kw)], [], [out])
+
+    def mm(out, lhsT, rhs, start, stop):
+        return lambda: g.tensor.matmul(out, lhsT, rhs, start, stop)
+
+    def wrap(bank, oc, strip, row, off=0, first=True, last=True, plus=()):
+        fns = []
+        rd = [X(strip, 0, 144), X(row, off, off + 1024)]
+        for j, (idm, buf, a) in enumerate(plus):
+            fns.append(mm(T[bank][:, oc:oc + 64], T[idm][:, 0:128], T[buf][:, a:a + 64], first and j == 0, False))
+            rd += [X(idm, 0, 128), X(buf, a, a + 64)]
+        for k in range(16):
+            fns.append(mm(T[bank][:, oc:oc + 64], T[strip][:, 16 - k:144 - k], T[row][:, off + k:off + 1024:16],
+                          first and not plus and k == 0, last and k == 15))
+        emit("P", fns, rd, [X(bank, oc, oc + 64)])
+
+    def full(bank, oc, terms, n, last=True, first=True):
+        fns = []
+        rd = []
+        for j, (idm, buf, a) in enumerate(terms):
+            fns.append(mm(T[bank][:, oc:oc + n], T[idm][:, 0:128], T[buf][:, a:a + n], first and j == 0, last and j == len(terms) - 1))
+            rd += [X(idm, 0, 128), X(buf, a, a + n)]
+        emit("P", fns, rd, [X(bank, oc, oc + n)])
+
+    def spread(banks, parts, first, last):
+        for h in range(2):
+            fns = []
+            rd = [X("ES", 0, 2304)]
+            for j, (part, buf, col) in enumerate(parts):
+                for k in range(8 * h, 8 * h + 8):
+                    fns.append(mm(T[banks[h]][:, 64 * (k % 8):64 * (k % 8) + 64], T.ES[:, 144 * k + 16 - part:144 * k + 144 - part],
+                                  T[buf][:, col:col + 64], first and j == 0 and k % 8 == 0,
+                                  last and j == len(parts) - 1 and k % 8 == 7))
+                rd.append(X(buf, col, col + 64))
+            emit("P", fns, rd, [X(banks[h], 0, 512)])
+
+    dma("S", T.hl[:, 0:V0], T.h0[:, I:I + V0], [], [X("hl", 0, V0)])
+    dma("A", T.si[:, 0:42], T.sl[:, :], [], [X("si", 0, 42)])
+    dma("S", T.KI[:, 0:64], T.kl[:, :], [], [X("KI", 0, 64)])
+    dma("A", T.KI[:, 64:128], T.kr[:, :], [], [X("KI", 64, 128)])
+    dma("S", T.vi[:, 0:V0], T.vel[:, :], [], [X("vi", 0, V0)])
+    dma("S", T.hi[:, :], T.h0[:, 0:I], [], [X("hi", 0, 1024)])
+
+    vset(X("ones", 0, 144), 1.0)
+    giota(X("pi", 0, 1), [[0, 1]], 0, 1, False)
+    giota(X("jr", 0, 16), [[1, 16]], 0, 0, True)
+    gsel(X("ec", 0, 144), X("ones", 0, 144), [[-1, 16], [-16, 9]], OP.is_equal, 16, 1)
+    gsel(X("bc", 0, 9), X("ones", 0, 9), [[-16, 9]], OP.is_ge, 16, 1)
+    gsel(X("bc", 0, 9), X("bc", 0, 9), [[16, 9]], OP.is_ge, -1, -1)
+    gsel(X("id1", 0, 128), X("ones", 0, 128), [[-1, 128]], OP.is_equal, 0, 1)
+    giota(X("c16", 0, 128), [[0, 2], [16, 64]], 0, 0, True)
+    giota(X("nrow", 0, 1024), [[1, 1024]], 0, 0, True)
+    vset(X("BS", 0, 144), 0.0)
+    vset(X("ES", 0, 2304), 0.0)
+    vts(X("pq", 0, 1), X("pi", 0, 1), 15, OP.bitwise_and)
+    vcopy(X("qf", 0, 1), X("pq", 0, 1))
+    vts(X("oh", 0, 16), X("jr", 0, 16), X("qf", 0, 1), OP.is_equal)
+    vts(X("NN", 0, 128), X("c16", 0, 128), X("qf", 0, 1), OP.add)
+    vcopy(X("BS", 0, 144, 16), X("bc", 0, 9))
+    vcopy(X("ES", 0, 2304, 16), X("ec", 0, 144))
+    vcopy(X("HA", I, I + V0), X("hl", 0, V0))
+    vcopy(X("su", 0, 42), X("si", 0, 42))
+    act(X("sh", 0, 672), ind(X("HA", I, I + V0), X("su", 0, 42)))
+    vcopy(X("KU", 0, 128), X("KI", 0, 128))
+    vset(X("PW", 0, 1024), 1088.0)
+    vcopy(X("vo", 0, V0), X("vi", 0, V0))
+    act(X("sv", 0, 672), ind(X("vo", 0, V0), X("su", 0, 42)))
+
+    mine = sends(T, topo, rank)
+    nsent = 0
+    for buf, land, sem in (("sh", "lh", "arrH"), ("sv", "lv", "arrV")):
+        sync("G", hazards("G", [X(buf, 0, 672)], []))
+        tr = []
+        for d in range(1, 8):
+            rid, pid, _ = topo.addr(T.cores[(rank + d) % 8])
+            tr.append(RemoteDMATransfer(src=T[buf][:, GH * (d - 1):GH * d], dst=T[land][:, GH * (d - 1):GH * d],
+                                        dst_ids=[DstId(rid=rid, pnc=pid)], dma_engine_mask=sum(1 << e for e in mine[d]),
+                                        remote_sem=T.sem[sem]))
+            nsent += len(mine[d])
+        g.remote_dma_fused(tr, local_sem=T.sem.sent)
+    narr = sum(len(sends(T, topo, (rank - d) % 8)[d]) for d in range(1, 8))
+    for land, sem in (("lh", "arrH"), ("lv", "arrV")):
+        cnt[sem] = narr
+        acc.setdefault(land, []).append((True, 0, 672, (sem, narr, "R", {})))
+
+    for j, a, w, b in ((0, ("oh", 0), 1.0, ("oh", 1)), (1, ("oh", 2), 16.0, ("oh", 3)), (2, ("oh", 4), 16.0, ("oh", 5)),
+                       (3, ("ww", 1), 1.0, ("ww", 2)), (4, ("oh", 1), 16.0, ("oh", 2)), (5, ("oh", 2), 64.0, ("oh", 1)),
+                       (6, ("oh", 3), 16.0, ("oh", 4)), (7, ("oh", 0), 1.0, ("oh", 0)), (8, ("oh", 2), 15.0, ("oh", 2))):
+        vts(X("ww", j, j + 1), X(a[0], a[1], a[1] + 1), w, OP.mult, X(b[0], b[1], b[1] + 1), OP.add)
+    for nm, w in (("sC32", ("oh", 0)), ("sG", ("ww", 0)), ("sL", ("ww", 1)), ("sR", ("ww", 2)), ("sS", ("ww", 3)), ("sC", ("oh", 0)),
+                  ("sC2", ("ww", 7)), ("sPn", ("ww", 4)), ("sPB", ("ww", 5)), ("sRC", ("ww", 6))):
+        act(X(nm, 0, 144), X("BS", 0, 144), scale=X(w[0], w[1], w[1] + 1))
+    act(X("BSn", 0, 144), X("BS", 0, 144), scale=-1.0)
+    for nm, w in (("idn", -1.0), ("idn16", -16.0), ("id64", 64.0), ("idk", 1024.0), ("id32", 1.0)):
+        act(X(nm, 0, 128), X("id1", 0, 128), scale=w)
+    act(X("nch", 0, 64), X("c16", 0, 64))
+    act(X("nch", 64, 128), X("c16", 0, 64), AF.Identity, 0.0, X("qf", 0, 1))
+    act(X("hcl", 1024, 2064), X("ES", 0, 1040), scale=0.0)
+    act(X("hcr", 1024, 2064), X("ES", 0, 1040), scale=0.0)
+    act(X("GW", 1024, LEAF), X("ES", 0, LEAF - 1024), scale=0.0)
+    act(X("CW", 1024, LEAF), X("ES", 0, LEAF - 1024), AF.Identity, 0.0, X("ww", 8, 9))
+    for j, c in enumerate((0.0, 0.5, 0.25, 0.75)):
+        vset(X("cq", 64 * j, 64 * j + 64), c)
+
+    def kchunks():
+        vts(X("CI", 0, 128), X("KI", 0, 128), 4, OP.arith_shift_right)
+        vts(X("CI", 128, 256), X("KI", 0, 128), 15, OP.bitwise_and)
+        vts(X("LF", 0, 128), X("KI", 0, 128), 1024, OP.is_ge)
+        vcopy(X("CK", 0, 256), X("CI", 0, 256))
+        vtt(X("TB", 0, 128), X("KI", 0, 128), X("NN", 0, 128), OP.is_gt)
+
+    def inner():
+        act(X("inn", 0, 128), X("LF", 0, 128), AF.Copy, -1.0, 1.0)
+
+    def kspread():
+        full("b7", 0, [("id1", "CK", 0), ("id64", "CK", 128), ("idk", "LF", 0)], 128)
+        spread(("b0", "b1"), [(2, "CK", 0), (3, "CK", 128), (4, "CK", 64), (5, "CK", 192)], True, False)
+
+    def pchunks():
+        vts(X("CIP", 0, 64), X("PI", 0, 64), 4, OP.arith_shift_right)
+        vts(X("CIP", 64, 128), X("PI", 0, 64), 15, OP.bitwise_and)
+        vtt(X("TB", 128, 192), X("PI", 0, 64), X("NN", 0, 64), OP.is_gt)
+        vcopy(X("CKP", 0, 128), X("CIP", 0, 128))
+        full("b6", 64, [("id1", "CKP", 0), ("id64", "CKP", 64), ("idk", "LFP", 0)], 64)
+        vcopy(X("PB", 0, 64), X("b6", 64, 128))
+
+    for a in (0, 1):
+        vcopy(ind(X("PW", 0, 2049), X("KU", 64 * a, 64 * a + 64)), X("nrow", 0, 1024))
+        if a == 0:
+            vcopy(X("HA", 0, I), X("hi", 0, I))
+            kchunks()
+            kspread()
+            vcopy(X("KB", 0, 128), X("b7", 0, 128))
+            inner()
+    wrap("b7", 192, "sC32", "PW")
+    vcopy(X("HA", I + V0, 2049), X("lh", 0, 672))
+
+    cur, nxt = "HA", "HB"
+    for r in range(RO):
+        last = r == RO - 1
+        win = X(cur, 0, 2049)
+        wl, wr = X("hcl", 0, 2049), X("hcr", 0, 2049)
+        act(X("hcl", 0, 1024), ind(win, X("KU", 0, 64)))
+        vcopy(X("hcr", 0, 1024), ind(win, X("KU", 64, 128)))
+        wrap("b4", 0, "BS", "hcl")
+        wrap("b4", 64, "BS", "hcr")
+        if r:
+            kchunks()
+            kspread()
+        act(X("zz", 0, 512), ind(wl, X("KU", 64, 96)))
+        act(X("zz", 512, 1024), ind(wl, X("KU", 96, 128)))
+        if r:
+            inner()
+        full("b2", 0, [("idn", "hcl", 0), ("id1", "zz", 0)], 512)
+        full("b3", 0, [("idn", "hcl", 512), ("id1", "zz", 512)], 512)
+        act(X("s4", 0, 64), X("b4", 0, 64), scale=-1.0)
+        act(X("hr2", 0, 1024), X("hcr", 0, 1024))
+        vtt(X("mm", 1024, 2048), ind(wr, X("KU", 64, 128)), X("hcl", 0, 1024), OP.max)
+        vtt(X("SUm", 0, 128), X("b4", 0, 128), X("inn", 0, 128), OP.mult)
+        full("b5", 0, [("id32", "SUm", 0), ("idn", "cq", 0)], 128, False)
+        full("b6", 0, [("id32", "SUm", 0), ("idn", "cq", 128)], 128, False)
+        full("b6", 64, [("id32", "s4", 0)], 64, False, False)
+        wrap("b5", 64, "BSn", "mm", 1024, False, False)
+        act(X("rl", 0, 512), X("b2", 0, 512), AF.Relu)
+        act(X("rl", 512, 1024), X("b3", 0, 512), AF.Relu)
+        vtt(X("mm", 2048, 3072), ind(wl, X("KU", 0, 64)), X("hcr", 0, 1024), OP.max)
+        if r:
+            vcopy(X("KB", 0, 128), X("b7", 0, 128))
+        wrap("b6", 64, "BSn", "rl", 0, False, False)
+        wrap("b6", 0, "BSn", "mm", 2048, False, True)
+        vtt(X("mm", 0, 1024), ind(wr, X("KU", 0, 64)), X("hr2", 0, 1024), OP.max)
+        if r:
+            act(X("cg", 512, 1024), ind(X("CW", 0, WIN), X("PPu", 32, 64)))
+        act(X("q1s", 0, 128), X("b6", 0, 128))
+
+        def leaves():
+            full("b2", 0, [("id1", cur, I), ("id1", "vo", 0)], V0)
+            act(X("y1", 0, V0), X("b2", 0, V0), AF.Relu, -1.0, 255.0)
+            if not last:
+                full("b3", 0, [("id1", cur, I + V0), ("id1", "lv", 0)], 336)
+                full("b4", 0, [("id1", cur, I + V0 + 336), ("id1", "lv", 336)], 336)
+                act(X("y1", V0, V0 + 336), X("b3", 0, 336), AF.Relu, -1.0, 255.0)
+                act(X("y1", V0 + 336, 1025), X("b4", 0, 336), AF.Relu, -1.0, 255.0)
+        if not r:
+            leaves()
+        wrap("b5", 0, "BSn", "mm", 0, False, True)
+        if r:
+            leaves()
+        vtt(X("qq", 0, 128), X("q1s", 0, 128), X("b5", 0, 128), OP.max)
+        vtt(X("ghi", 0, 64), X("qq", 0, 64), X("qq", 64, 128), OP.max)
+        vtt(X("ga", 0, 64), X("qq", 0, 64), X("qq", 64, 128), OP.max)
+        vtt(X("glo", 0, 64), X("ga", 0, 64), X("ghi", 0, 64), OP.subtract)
+        spread(("b0", "b1"), [(0, "ghi", 0), (1, "glo", 0)], False, True)
+        act(X("GW", 0, 512), X("b0", 0, 512))
+        act(X("GW", 512, 1024), X("b1", 0, 512))
+        gwin = X("GW", 0, WIN)
+
+        def gather(buf, lst, o, a, b, eng):
+            eng(X(buf, a, b), ind(gwin, X(lst, o + a // 16, o + b // 16)))
+
+        def xx(oc, strip, row, side):
+            wrap("b7", oc, strip, row, plus=[("idn16", "CK", 64 * side), ("idn", "CK", 128 + 64 * side)])
+        half = 0 if r else 512
+        gather("gl", "KB", 0, half, 1024, act)
+        gather("gr", "KB", 64, half, 1024, act)
+        P_ = X("PI", 0, 64)
+        if r:
+            wrap("b6", 128, "sC2", "cg", plus=[("idn", "ones", 0), ("idn", "ones", 0)])
+            wrap("b6", 192, "sRC", "cg", plus=[("idn16", "CKP", 0), ("idn", "CKP", 64)])
+        else:
+            vcopy(P_, X("b7", 192, 256))
+            vts(X("LFP", 0, 64), P_, 1024, OP.is_ge)
+            vts(X("LF16", 0, 64), P_, 1024, OP.is_ge, 16, OP.mult)
+        if not last:
+            spread(("b2", "b3"), [(3, "CK", 64), (4, "CK", 192), (2, "LF16", 0)], True, False)
+        if r:
+            def pt(i):
+                return X("pt", 64 * i, 64 * i + 64)
+            vtt(pt(1), X("ee", 0, 64), X("ee", 64, 128), OP.add)
+            vtt(pt(1), pt(0), pt(1), OP.subtract)
+            vtt(pt(2), X("b7", 256, 320), P_, OP.subtract)
+            vtt(pt(2), pt(1), pt(2), OP.mult)
+            vtt(pt(5), P_, pt(2), OP.add)
+            vtt(pt(3), X("b6", 128, 192), X("sd", 0, 64), OP.subtract)
+            vts(pt(4), X("b6", 192, 256), 0.0, OP.is_equal, 4.0, OP.mult)
+            vtt(pt(6), pt(3), pt(4), OP.is_equal)
+            vtt(pt(6), pt(6), X("GPs", 0, 64), OP.mult)
+            vtt(P_, pt(5), pt(6), OP.add)
+        pchunks()
+        if not r:
+            gather("gl", "KB", 0, 0, 512, vcopy)
+            gather("gr", "KB", 64, 0, 512, vcopy)
+        cut = 768 if r else 512
+        gather("gp", "PB", 0, 0, cut, vcopy)
+        gather("gp", "PB", 0, cut, 1024, act)
+        wrap("b4", 0, "sG", "gl", plus=[("id1", "TB", 0)])
+        xx(64, "sL", "gl", 1)
+        xx(192, "sR", "gl", 1)
+        wrap("b5", 0, "sG", "gr", plus=[("id1", "TB", 64)])
+        wrap("b6", 0, "sG", "gp", plus=[("id1", "TB", 128)])
+        if not last:
+            spread(("b2", "b3"), [(1, "CKP", 0), (2, "CKP", 64)], False, False)
+        vts(X("gi", 0, 64), X("ga", 0, 64), 0.375, OP.add)
+        vtt(X("cd", 0, 64), X("gi", 0, 64), X("ga", 0, 64), OP.subtract)
+        vts(X("cc", 0, 64), X("cd", 0, 64), 4.0, OP.mult, 1.0, OP.add)
+        vts(X("tt", 0, 64), X("b4", 0, 64), 1.0, OP.max)
+        vtt(X("tt", 64, 128), X("b5", 0, 64), X("tt", 0, 64), OP.max)
+        vtt(X("tt", 128, 192), X("b6", 0, 64), X("tt", 64, 128), OP.max)
+        vtt(X("rot", 0, 64), X("gi", 0, 64), X("tt", 128, 192), OP.is_ge)
+        vtt(X("code", 0, 64), X("rot", 0, 64), X("cc", 0, 64), OP.mult)
+        if last:
+            act(X("OH", I, I + V0), X("y1", 0, V0), AF.Relu, -1.0, 255.0)
+            dma("S", T.yh[:, I:I + V0], T.OH[:, I:I + V0], [X("OH", I, I + V0)], [])
+        else:
+            act(X(nxt, I, 2049), X("y1", 0, 1025), AF.Relu, -1.0, 255.0)
+        xx(0, "sL", "gr", 0)
+        spread(("b2", "b3"), [(0, "code", 0)], last, True)
+        xx(128, "sR", "gr", 0)
+        wrap("b7", 320, "sR", "gp", plus=[("idn", "nch", 0), ("idn", "nch", 64)])
+        wrap("b7", 256, "sS", "gp", plus=[("idn", "nch", 0), ("idn", "nch", 64)])
+        for j, c in enumerate((3, 1, 4, 2)):
+            vts(X("MK", 64 * j, 64 * j + 64), X("code", 0, 64), float(c), OP.is_equal)
+        act(X("CW", 0, 512), X("b2", 0, 512))
+        vcopy(X("CW", 512, 1024), X("b3", 0, 512))
+        cwin = X("CW", 0, WIN)
+        vcopy(X("cp", 0, 512), ind(cwin, X("PB", 0, 32)))
+        act(X("cp", 512, 1024), ind(cwin, X("PB", 32, 64)))
+        wrap("b5", 0, "sC", "cp", plus=[("idn", "ones", 0)])
+        if not last:
+            wrap("b4", 0, "sPB", "cp")
+            wrap("b4", 64, "sPn", "cp", plus=[("idn16", "CKP", 0), ("idn", "CKP", 64)])
+        vtt(X("pr", 0, 256), X("b7", 0, 256), X("MK", 0, 256), OP.mult)
+        vts(X("sd", 0, 64), X("b7", 320, 384), 0.0, OP.is_equal, 2.0, OP.mult)
+        vtt(X("xs", 0, 128), X("pr", 0, 128), X("pr", 128, 256), OP.add)
+        vts(X("sd", 64, 128), X("sd", 0, 64), 1.0, OP.add)
+        vtt(X("K1", 0, 128), X("KI", 0, 128), X("xs", 0, 128), OP.add)
+        vtt(X("dS", 0, 64), X("b7", 256, 320), X("K1", 0, 64), OP.subtract)
+        vtt(X("dS", 64, 128), X("b7", 256, 320), X("K1", 64, 128), OP.subtract)
+        vtt(X("ee", 0, 64), X("b5", 0, 64), X("sd", 0, 64), OP.is_equal)
+        vtt(X("ee", 64, 128), X("b5", 0, 64), X("sd", 64, 128), OP.is_equal)
+        vtt(X("te", 0, 128), X("ee", 0, 128), X("dS", 0, 128), OP.mult)
+        vtt(X("KI", 0, 128), X("K1", 0, 128), X("te", 0, 128), OP.add)
+        vcopy(X("KU", 0, 128), X("KI", 0, 128))
+        act(X("rr", 0, 672), ind(win, X("KU", 64, 106)))
+        if last:
+            vts(X("CI", 0, 128), X("KI", 0, 128), 15, OP.bitwise_and)
+            vtt(X("fh", 0, 128), X("KI", 0, 128), X("CI", 0, 128), OP.subtract)
+            vcopy(X("fl", 0, 128), X("CI", 0, 128))
+        vcopy(X("rr", 672, 1024), ind(win, X("KU", 106, 128)))
+        if not last:
+            vts(X("pt", 0, 64), X("b5", 0, 64), 0.0, OP.is_ge)
+            vcopy(X("PPu", 0, 64), X("b4", 0, 64))
+            vcopy(X("GPs", 0, 64), X("b4", 64, 128))
+            act(X("cg", 0, 512), ind(cwin, X("PPu", 0, 32)))
+        dst = "OH" if last else nxt
+        vtt(X(dst, 672, 1024), ind(win, X("KU", 42, 64)), X("rr", 672, 1024), OP.max)
+        if last:
+            dma("S", T.yh[:, 672:1024], T.OH[:, 672:1024], [X("OH", 672, 1024)], [])
+        vtt(X(dst, 0, 672), ind(win, X("KU", 0, 42)), X("rr", 0, 672), OP.max)
+        if last:
+            dma("S", T.yh[:, 0:672], T.OH[:, 0:672], [X("OH", 0, 672)], [])
+        cur, nxt = nxt, cur
+
+    for h in range(2):
+        fns = []
+        for j, (part, buf) in enumerate(((0, "fh"), (0, "fl"), (1, "fh"), (1, "fl"))):
+            for k in range(16):
+                c = 64 * part + 32 * h
+                fns.append(mm(T["b%d" % h][:, k:512:16], T.ES[:, 144 * k + 16 - part:144 * k + 144 - part], T[buf][:, c:c + 32],
+                              j == 0 and k == 0, j == 3 and k == 15))
+        emit("P", fns, [X("ES", 0, 2304), X("fh", 0, 128), X("fl", 0, 128)], [X("b%d" % h, 0, 512)])
+        act(X("OK", 512 * h, 512 * h + 512), X("b%d" % h, 0, 512))
+        for a in range(2):
+            dma("A", T.yk[:, 1024 * a + 512 * h:1024 * a + 512 * h + 512], T.OK[a::16, 512 * h:512 * h + 512],
+                [X("OK", 512 * h, 512 * h + 512)], [])
+    cnt["sent"] = nsent
+    for s, c in cnt.items():
+        g.wait_ge(T.sem[s], c)

@@ -4,19 +4,20 @@ from concourse.mybir import AluOpType, ActivationFunctionType
 OP = AluOpType
 AF = ActivationFunctionType
 I, V0, GH, RO = 1024, 353, 96, 3
-LEAF, WIN = 2120, 2113
+LEAF = WIN = 2176
 
 SCRATCH = {"b%d" % _b: ("psum", [128, 512], "float32") for _b in range(8)}
 for _dt, _names in (
-        ("int32", "hl 360 hi 1024 vi 360 si 48 pi 8 pq 8 KI 128 CI 256 PI 64 CIP 128 gi 64"),
+        ("int32", "hl 360 hi 1024 vi 360 si 48 pi 8 pq 8 KI 128 gi 64"),
         ("uint16", "su 48 KU 128 KB 128 PB 64 PPu 64"),
-        ("bfloat16", "HA 2064 HB 2064 vo 368 sh 672 sv 672 lh 672 lv 672 hcl 2064 hcr 2064 hr2 1024 mm 3072 zz 1024 rl 1024 rr 1024 "
-                     "GW 2120 CW 2120 gl 1024 gr 1024 gp 1024 cp 1024 cg 1024 ones 144 ec 144 ES 2304 bc 16 BS 144 BSn 144 sG 144 sL 144 "
-                     "sR 144 sS 144 sC 144 sC2 144 sPn 144 sPB 144 sRC 144 id1 128 idn 128 idn16 128 id64 128 idk 128 CK 256 LF 128 "
-                     "TB 192 CKP 128 LFP 64 LF16 64 ghi 64 glo 64 code 64 fh 128 fl 128 nch 128 cq 256"),
-        ("float32", "y1 1032 PW 2056 nrow 1024 sC32 144 id32 128 qf 8 jr 16 oh 16 ww 16 c16 128 NN 128 inn 128 GPs 64 SUm 128 "
-                    "q1s 128 qq 128 ga 64 cd 64 cc 64 tt 192 rot 64 MK 256 pr 256 xs 128 K1 128 dS 128 sd 128 ee 128 te 128 "
-                    "pt 512 s4 64 OK 1024 OH 1384")):
+        ("bfloat16", "HA 2064 HB 2064 vo 368 sh 672 sv 672 lh 672 lv 672 hcl 2176 hcr 2176 hr2 1024 mm 3072 zz 1024 rl 1024 rr 1024 "
+                     "GW 2176 CW 2176 gl 1024 gr 1024 gp 1024 cp 1024 cg 1024 ones 144 ec 144 ES 2304 bc 16 BS 144 BSn 144 sG 144 sL 144 "
+                     "sR 144 sS 144 sC 144 sC2 144 sPn 144 sPB 144 sRC 144 sO 144 id1 128 idn 128 idn16 128 id16 128 id64 128 id512 128 "
+                     "idnb 128 idh 128 idp 128 PW 2064 nrow 1024 chi 64 k129 64 sgn 128 CK 256 "
+                     "TB 192 CKP 128 ghi 64 glo 64 code 64 fh 128 fl 128 nch 128 cq 256"),
+        ("float32", "y1 1032 id32 128 qf 8 jr 16 oh 16 ww 16 c16 64 KF 128 PI 64 GPs 64 sib 64 sp 64 "
+                    "q1s 128 qm 128 qq 128 ga 64 cd 64 cc 64 tt 192 rot 64 MK 256 pr 256 xs 128 K1 128 dS 128 sd 128 ee 128 te 128 "
+                    "pt 512 OK 2048 OH 1384")):
     _w = _names.split()
     for _n, _c in zip(_w[::2], _w[1::2]):
         SCRATCH[_n] = ("sbuf", [128, int(_c)], _dt)
@@ -186,17 +187,16 @@ def rank_program(g, core, T, topo):
             rd += [X(idm, 0, 128), X(buf, a, a + n)]
         emit("P", fns, rd, [X(bank, oc, oc + n)])
 
-    def spread(banks, parts, first, last):
-        for h in range(2):
-            fns = []
-            rd = [X("ES", 0, 2304)]
-            for j, (part, buf, col) in enumerate(parts):
-                for k in range(8 * h, 8 * h + 8):
-                    fns.append(mm(T[banks[h]][:, 64 * (k % 8):64 * (k % 8) + 64], T.ES[:, 144 * k + 16 - part:144 * k + 144 - part],
-                                  T[buf][:, col:col + 64], first and j == 0 and k % 8 == 0,
-                                  last and j == len(parts) - 1 and k % 8 == 7))
-                rd.append(X(buf, col, col + 64))
-            emit("P", fns, rd, [X(banks[h], 0, 512)])
+    def spread1(banks, h, parts, first, last):
+        fns = []
+        rd = [X("ES", 0, 2304)]
+        for j, (part, buf, col) in enumerate(parts):
+            for k in range(8 * h, 8 * h + 8):
+                fns.append(mm(T[banks[h]][:, 64 * (k % 8):64 * (k % 8) + 64], T.ES[:, 144 * k + 16 - part:144 * k + 144 - part],
+                              T[buf][:, col:col + 64], first and j == 0 and k % 8 == 0,
+                              last and j == len(parts) - 1 and k % 8 == 7))
+            rd.append(X(buf, col, col + 64))
+        emit("P", fns, rd, [X(banks[h], 0, 512)])
 
     dma("S", T.hl[:, 0:V0], T.h0[:, I:I + V0], [], [X("hl", 0, V0)])
     dma("A", T.si[:, 0:42], T.sl[:, :], [], [X("si", 0, 42)])
@@ -212,27 +212,28 @@ def rank_program(g, core, T, topo):
     gsel(X("bc", 0, 9), X("ones", 0, 9), [[-16, 9]], OP.is_ge, 16, 1)
     gsel(X("bc", 0, 9), X("bc", 0, 9), [[16, 9]], OP.is_ge, -1, -1)
     gsel(X("id1", 0, 128), X("ones", 0, 128), [[-1, 128]], OP.is_equal, 0, 1)
-    giota(X("c16", 0, 128), [[0, 2], [16, 64]], 0, 0, True)
-    giota(X("nrow", 0, 1024), [[1, 1024]], 0, 0, True)
+    giota(X("c16", 0, 64), [[16, 64]], 0, 0, True)
+    giota(X("chi", 0, 64), [[1, 64]], 129, 0, True)
     vset(X("BS", 0, 144), 0.0)
     vset(X("ES", 0, 2304), 0.0)
     vts(X("pq", 0, 1), X("pi", 0, 1), 15, OP.bitwise_and)
     vcopy(X("qf", 0, 1), X("pq", 0, 1))
     vts(X("oh", 0, 16), X("jr", 0, 16), X("qf", 0, 1), OP.is_equal)
-    vts(X("NN", 0, 128), X("c16", 0, 128), X("qf", 0, 1), OP.add)
     vcopy(X("BS", 0, 144, 16), X("bc", 0, 9))
     vcopy(X("ES", 0, 2304, 16), X("ec", 0, 144))
     vcopy(X("HA", I, I + V0), X("hl", 0, V0))
     vcopy(X("su", 0, 42), X("si", 0, 42))
+    act(X("nch", 64, 128), X("c16", 0, 64), AF.Identity, 0.0, X("qf", 0, 1))
     act(X("sh", 0, 672), ind(X("HA", I, I + V0), X("su", 0, 42)))
     vcopy(X("KU", 0, 128), X("KI", 0, 128))
-    vset(X("PW", 0, 1024), 1088.0)
     vcopy(X("vo", 0, V0), X("vi", 0, V0))
-    act(X("sv", 0, 672), ind(X("vo", 0, V0), X("su", 0, 42)))
+    vts(X("ww", 11, 12), X("oh", 0, 1), 256.0, OP.mult)
+    vts(X("ww", 9, 10), X("oh", 1, 2), 16.0, OP.mult, X("ww", 11, 12), OP.add)
 
     mine = sends(T, topo, rank)
-    nsent = 0
-    for buf, land, sem in (("sh", "lh", "arrH"), ("sv", "lv", "arrV")):
+    nsent = [0]
+
+    def exchange(buf, land, sem):
         sync("G", hazards("G", [X(buf, 0, 672)], []))
         tr = []
         for d in range(1, 8):
@@ -240,63 +241,82 @@ def rank_program(g, core, T, topo):
             tr.append(RemoteDMATransfer(src=T[buf][:, GH * (d - 1):GH * d], dst=T[land][:, GH * (d - 1):GH * d],
                                         dst_ids=[DstId(rid=rid, pnc=pid)], dma_engine_mask=sum(1 << e for e in mine[d]),
                                         remote_sem=T.sem[sem]))
-            nsent += len(mine[d])
+            nsent[0] += len(mine[d])
         g.remote_dma_fused(tr, local_sem=T.sem.sent)
+    exchange("sh", "lh", "arrH")
+
+    act(X("PW", 0, 1024), X("ES", 0, 1024), AF.Identity, 0.0, X("ww", 9, 10))
+    for h in range(2):
+        fns = []
+        for part, buf, col in ((0, "chi", 0), (1, "nch", 64)):
+            for k in range(16):
+                c = col + 32 * h
+                fns.append(mm(T["b%d" % h][:, k:512:16], T.ES[:, 144 * k + 16 - part:144 * k + 144 - part], T[buf][:, c:c + 32],
+                              part == 0 and k == 0, part == 1 and k == 15))
+        emit("P", fns, [X("ES", 0, 2304), X("chi", 0, 64), X("nch", 64, 128)], [X("b%d" % h, 0, 512)])
+    act(X("nrow", 0, 512), X("b0", 0, 512))
+    act(X("nrow", 512, 1024), X("b1", 0, 512))
+    act(X("sv", 0, 672), ind(X("vo", 0, V0), X("su", 0, 42)))
+    exchange("sv", "lv", "arrV")
     narr = sum(len(sends(T, topo, (rank - d) % 8)[d]) for d in range(1, 8))
     for land, sem in (("lh", "arrH"), ("lv", "arrV")):
         cnt[sem] = narr
         acc.setdefault(land, []).append((True, 0, 672, (sem, narr, "R", {})))
 
+    def scatter(a):
+        vcopy(ind(X("PW", 0, 2049), X("KU", a, a + 64)), X("nrow", 0, 1024))
+
+    vts(X("ww", 10, 11), X("oh", 1, 2), 129.0, OP.mult)
     for j, a, w, b in ((0, ("oh", 0), 1.0, ("oh", 1)), (1, ("oh", 2), 16.0, ("oh", 3)), (2, ("oh", 4), 16.0, ("oh", 5)),
                        (3, ("ww", 1), 1.0, ("ww", 2)), (4, ("oh", 1), 16.0, ("oh", 2)), (5, ("oh", 2), 64.0, ("oh", 1)),
-                       (6, ("oh", 3), 16.0, ("oh", 4)), (7, ("oh", 0), 1.0, ("oh", 0)), (8, ("oh", 2), 15.0, ("oh", 2))):
+                       (6, ("oh", 3), 16.0, ("oh", 4)), (7, ("oh", 0), 1.0, ("oh", 0)), (8, ("oh", 2), 16.0, ("ww", 10))):
         vts(X("ww", j, j + 1), X(a[0], a[1], a[1] + 1), w, OP.mult, X(b[0], b[1], b[1] + 1), OP.add)
-    for nm, w in (("sC32", ("oh", 0)), ("sG", ("ww", 0)), ("sL", ("ww", 1)), ("sR", ("ww", 2)), ("sS", ("ww", 3)), ("sC", ("oh", 0)),
-                  ("sC2", ("ww", 7)), ("sPn", ("ww", 4)), ("sPB", ("ww", 5)), ("sRC", ("ww", 6))):
-        act(X(nm, 0, 144), X("BS", 0, 144), scale=X(w[0], w[1], w[1] + 1))
-    act(X("BSn", 0, 144), X("BS", 0, 144), scale=-1.0)
-    for nm, w in (("idn", -1.0), ("idn16", -16.0), ("id64", 64.0), ("idk", 1024.0), ("id32", 1.0)):
+    vcopy(X("KF", 0, 128), X("KI", 0, 128))
+    vcopy(X("HA", 0, I), X("hi", 0, I))
+    for nm, w in (("idn", -1.0), ("idn16", -16.0), ("id64", 64.0), ("id32", 1.0), ("id512", 512.0), ("idnb", -4096.0),
+                  ("idh", 0.5), ("id16", 16.0)):
         act(X(nm, 0, 128), X("id1", 0, 128), scale=w)
     act(X("nch", 0, 64), X("c16", 0, 64))
-    act(X("nch", 64, 128), X("c16", 0, 64), AF.Identity, 0.0, X("qf", 0, 1))
-    act(X("hcl", 1024, 2064), X("ES", 0, 1040), scale=0.0)
-    act(X("hcr", 1024, 2064), X("ES", 0, 1040), scale=0.0)
-    act(X("GW", 1024, LEAF), X("ES", 0, LEAF - 1024), scale=0.0)
-    act(X("CW", 1024, LEAF), X("ES", 0, LEAF - 1024), AF.Identity, 0.0, X("ww", 8, 9))
+    gsel(X("idp", 0, 128), X("ones", 0, 128), [[-1, 16], [-16, 8]], OP.is_equal, 0, 1)
+    for nm in ("hcl", "hcr", "GW"):
+        giota(X(nm, 1024, LEAF), [[0, LEAF - 1024]], 0, 0, True)
+    act(X("BSn", 0, 144), X("BS", 0, 144), scale=-1.0)
     for j, c in enumerate((0.0, 0.5, 0.25, 0.75)):
         vset(X("cq", 64 * j, 64 * j + 64), c)
+    vset(X("k129", 0, 64), 129.0)
+    for nm, w in (("sG", ("ww", 0)), ("sL", ("ww", 1)), ("sR", ("ww", 2)), ("sS", ("ww", 3)), ("sC", ("oh", 0)), ("sO", ("oh", 1)),
+                  ("sC2", ("ww", 7)), ("sPn", ("ww", 4)), ("sPB", ("ww", 5)), ("sRC", ("ww", 6))):
+        act(X(nm, 0, 144), X("BS", 0, 144), scale=X(w[0], w[1], w[1] + 1))
 
-    def kchunks():
-        vts(X("CI", 0, 128), X("KI", 0, 128), 4, OP.arith_shift_right)
-        vts(X("CI", 128, 256), X("KI", 0, 128), 15, OP.bitwise_and)
-        vts(X("LF", 0, 128), X("KI", 0, 128), 1024, OP.is_ge)
-        vcopy(X("CK", 0, 256), X("CI", 0, 256))
-        vtt(X("TB", 0, 128), X("KI", 0, 128), X("NN", 0, 128), OP.is_gt)
+    P_ = X("PI", 0, 64)
+    OWN = [("idn", "nch", 0), ("idn", "nch", 64)]
+    TIE = ("idh", "ones", 0)
 
-    def inner():
-        act(X("inn", 0, 128), X("LF", 0, 128), AF.Copy, -1.0, 1.0)
+    def pt(i):
+        return X("pt", 64 * i, 64 * i + 64)
 
-    def kspread():
-        full("b7", 0, [("id1", "CK", 0), ("id64", "CK", 128), ("idk", "LF", 0)], 128)
-        spread(("b0", "b1"), [(2, "CK", 0), (3, "CK", 128), (4, "CK", 64), (5, "CK", 192)], True, False)
+    def chunks():
+        vts(X("CK", 0, 128), X("KF", 0, 128), 0.0625, OP.mult, 128.53125, OP.add)
+        full("b4", 128, [("id32", "KF", 0), ("idn16", "CK", 0)], 128)
+        full("b4", 256, [("id32", "KF", 0)] + OWN, 64)
+        full("b4", 320, [("id32", "KF", 64)] + OWN, 64)
+        for h in range(2):
+            spread1(("b0", "b1"), h, [(2, "CK", 0), (4, "CK", 64)], True, False)
 
-    def pchunks():
-        vts(X("CIP", 0, 64), X("PI", 0, 64), 4, OP.arith_shift_right)
-        vts(X("CIP", 64, 128), X("PI", 0, 64), 15, OP.bitwise_and)
-        vtt(X("TB", 128, 192), X("PI", 0, 64), X("NN", 0, 64), OP.is_gt)
-        vcopy(X("CKP", 0, 128), X("CIP", 0, 128))
-        full("b6", 64, [("id1", "CKP", 0), ("id64", "CKP", 64), ("idk", "LFP", 0)], 64)
-        vcopy(X("PB", 0, 64), X("b6", 64, 128))
-
-    for a in (0, 1):
-        vcopy(ind(X("PW", 0, 2049), X("KU", 64 * a, 64 * a + 64)), X("nrow", 0, 1024))
-        if a == 0:
-            vcopy(X("HA", 0, I), X("hi", 0, I))
-            kchunks()
-            kspread()
-            vcopy(X("KB", 0, 128), X("b7", 0, 128))
-            inner()
-    wrap("b7", 192, "sC32", "PW")
+    scatter(0)
+    chunks()
+    act(X("CK", 128, 256), X("b4", 128, 256), scale=1.0, bias=2064.0)
+    act(X("CW", 1024, LEAF), X("ES", 0, LEAF - 1024), AF.Identity, 0.0, X("ww", 8, 9))
+    scatter(64)
+    wrap("b6", 128, "sC", "PW")
+    wrap("b6", 192, "sO", "PW")
+    vcopy(X("CKP", 0, 128), X("b6", 128, 256))
+    full("b6", 0, [("id16", "CKP", 0), ("id1", "CKP", 64)], 64)
+    full("b6", 64, [("id1", "CKP", 0), ("id64", "CKP", 64)], 64)
+    full("b6", 384, [("id16", "CKP", 0), ("id1", "CKP", 64), ("idn16", "k129", 0)] + OWN, 64)
+    vts(X("PB", 0, 64), X("b6", 64, 128), -129.0, OP.add)
+    act(P_, X("b6", 0, 64), scale=1.0, bias=-2064.0)
+    act(X("TB", 128, 192), X("b6", 384, 448), AF.Sign)
     vcopy(X("HA", I + V0, 2049), X("lh", 0, 672))
 
     cur, nxt = "HA", "HB"
@@ -306,57 +326,82 @@ def rank_program(g, core, T, topo):
         wl, wr = X("hcl", 0, 2049), X("hcr", 0, 2049)
         act(X("hcl", 0, 1024), ind(win, X("KU", 0, 64)))
         vcopy(X("hcr", 0, 1024), ind(win, X("KU", 64, 128)))
-        wrap("b4", 0, "BS", "hcl")
-        wrap("b4", 64, "BS", "hcr")
+        act(X("sgn", 0, 128), X("CK", 0, 128), AF.Sign, 1.0, -192.5)
+        act(X("TB", 0, 128), X("b4", 256, 384), AF.Sign)
+        for h in range(2):
+            spread1(("b0", "b1"), h, [(3, "CK", 128), (5, "CK", 192)], False, False)
         if r:
-            kchunks()
-            kspread()
+            wrap("b7", 128, "sC2", "cg", plus=[("idn", "ones", 0), ("idn", "ones", 0)])
+            wrap("b7", 192, "sRC", "cg", plus=[("idn16", "CKP", 0), ("idn", "CKP", 64)])
+        wrap("b4", 0, "BS", "hcl", 0, True, False)
+        full("b6", 0, [("idn", "cq", 128)], 128, False)
+        wrap("b6", 64, "BSn", "hcl", 0, False, False)
+        wrap("b4", 64, "BS", "hcr", 0, False, False)
+        full("b4", 0, [("idnb", "sgn", 0), ("idnb", "ones", 0)], 128, True, False)
+        full("b7", 0, [("id1", "CK", 0), ("id64", "CK", 128), ("id512", "sgn", 0)], 128)
         act(X("zz", 0, 512), ind(wl, X("KU", 64, 96)))
         act(X("zz", 512, 1024), ind(wl, X("KU", 96, 128)))
-        if r:
-            inner()
+        vtt(X("mm", 1024, 2048), ind(wr, X("KU", 64, 128)), X("hcl", 0, 1024), OP.max)
         full("b2", 0, [("idn", "hcl", 0), ("id1", "zz", 0)], 512)
         full("b3", 0, [("idn", "hcl", 512), ("id1", "zz", 512)], 512)
-        act(X("s4", 0, 64), X("b4", 0, 64), scale=-1.0)
         act(X("hr2", 0, 1024), X("hcr", 0, 1024))
-        vtt(X("mm", 1024, 2048), ind(wr, X("KU", 64, 128)), X("hcl", 0, 1024), OP.max)
-        vtt(X("SUm", 0, 128), X("b4", 0, 128), X("inn", 0, 128), OP.mult)
-        full("b5", 0, [("id32", "SUm", 0), ("idn", "cq", 0)], 128, False)
-        full("b6", 0, [("id32", "SUm", 0), ("idn", "cq", 128)], 128, False)
-        full("b6", 64, [("id32", "s4", 0)], 64, False, False)
-        wrap("b5", 64, "BSn", "mm", 1024, False, False)
         act(X("rl", 0, 512), X("b2", 0, 512), AF.Relu)
         act(X("rl", 512, 1024), X("b3", 0, 512), AF.Relu)
+        full("b5", 0, [("idn", "cq", 0)], 128, False)
         vtt(X("mm", 2048, 3072), ind(wl, X("KU", 0, 64)), X("hcr", 0, 1024), OP.max)
-        if r:
-            vcopy(X("KB", 0, 128), X("b7", 0, 128))
+        wrap("b5", 64, "BSn", "mm", 1024, False, False)
         wrap("b6", 64, "BSn", "rl", 0, False, False)
-        wrap("b6", 0, "BSn", "mm", 2048, False, True)
         vtt(X("mm", 0, 1024), ind(wr, X("KU", 0, 64)), X("hr2", 0, 1024), OP.max)
-        if r:
-            act(X("cg", 512, 1024), ind(X("CW", 0, WIN), X("PPu", 32, 64)))
+        wrap("b6", 0, "BSn", "mm", 2048, False, True)
         act(X("q1s", 0, 128), X("b6", 0, 128))
-
-        def leaves():
-            full("b2", 0, [("id1", cur, I), ("id1", "vo", 0)], V0)
-            act(X("y1", 0, V0), X("b2", 0, V0), AF.Relu, -1.0, 255.0)
-            if not last:
-                full("b3", 0, [("id1", cur, I + V0), ("id1", "lv", 0)], 336)
-                full("b4", 0, [("id1", cur, I + V0 + 336), ("id1", "lv", 336)], 336)
-                act(X("y1", V0, V0 + 336), X("b3", 0, 336), AF.Relu, -1.0, 255.0)
-                act(X("y1", V0 + 336, 1025), X("b4", 0, 336), AF.Relu, -1.0, 255.0)
-        if not r:
-            leaves()
         wrap("b5", 0, "BSn", "mm", 0, False, True)
+        full("b2", 0, [("id1", cur, I), ("id1", "vo", 0)], V0)
+        act(X("y1", 0, V0), X("b2", 0, V0), AF.Relu, -1.0, 255.0)
+        if not last:
+            full("b3", 0, [("id1", cur, I + V0), ("id1", "lv", 0)], 336)
+            full("b6", 128, [("id1", cur, I + V0 + 336), ("id1", "lv", 336)], 336)
+            act(X("y1", V0, V0 + 336), X("b3", 0, 336), AF.Relu, -1.0, 255.0)
+            act(X("y1", V0 + 336, 1025), X("b6", 128, 464), AF.Relu, -1.0, 255.0)
+        vts(X("KB", 0, 128), X("b7", 0, 128), 383.0, OP.add)
         if r:
-            leaves()
-        vtt(X("qq", 0, 128), X("q1s", 0, 128), X("b5", 0, 128), OP.max)
+            vtt(pt(1), X("ee", 0, 64), X("ee", 64, 128), OP.add)
+            vtt(pt(3), X("b7", 128, 192), X("sd", 0, 64), OP.subtract)
+            vts(pt(4), X("b7", 192, 256), 0.0, OP.is_equal, 4.0, OP.mult)
+            vtt(pt(2), X("sib", 0, 64), P_, OP.subtract)
+            vtt(pt(1), pt(0), pt(1), OP.subtract)
+            vtt(pt(6), pt(3), pt(4), OP.is_equal)
+        vtt(X("qm", 0, 128), X("q1s", 0, 128), X("b5", 0, 128), OP.max)
+        vtt(X("qq", 0, 128), X("b4", 0, 128), X("qm", 0, 128), OP.add)
         vtt(X("ghi", 0, 64), X("qq", 0, 64), X("qq", 64, 128), OP.max)
         vtt(X("ga", 0, 64), X("qq", 0, 64), X("qq", 64, 128), OP.max)
         vtt(X("glo", 0, 64), X("ga", 0, 64), X("ghi", 0, 64), OP.subtract)
-        spread(("b0", "b1"), [(0, "ghi", 0), (1, "glo", 0)], False, True)
+        for part, buf in ((0, "ghi"), (1, "glo")):
+            for h in range(2):
+                spread1(("b0", "b1"), h, [(part, buf, 0)], False, part == 1)
+        if not last:
+            spread1(("b2", "b3"), 0, [(3, "CK", 64), (4, "CK", 192)], True, False)
+        if r:
+            vtt(pt(2), pt(1), pt(2), OP.mult)
+            vtt(pt(6), pt(6), X("GPs", 0, 64), OP.mult)
+            vtt(pt(5), P_, pt(2), OP.add)
+            vtt(P_, pt(5), pt(6), OP.add)
+            vts(X("CKP", 0, 64), P_, 0.0625, OP.mult, 128.53125, OP.add)
+            full("b7", 320, [("id32", "PI", 0), ("idn16", "CKP", 0)], 64)
+            full("b7", 384, [("id32", "PI", 0)] + OWN, 64)
+        vts(X("gi", 0, 64), X("ga", 0, 64), 0.375, OP.add)
+        vtt(X("cd", 0, 64), X("gi", 0, 64), X("ga", 0, 64), OP.subtract)
+        if not last:
+            spread1(("b2", "b3"), 1, [(3, "CK", 64), (4, "CK", 192)], True, False)
+        if r:
+            vts(X("CKP", 64, 128), X("b7", 320, 384), 2064.0, OP.add)
+            full("b7", 320, [("id1", "CKP", 0), ("id64", "CKP", 64)], 64)
+        vts(X("cc", 0, 64), X("cd", 0, 64), 4.0, OP.mult, 1.0, OP.add)
         act(X("GW", 0, 512), X("b0", 0, 512))
-        act(X("GW", 512, 1024), X("b1", 0, 512))
+        if not r:
+            vcopy(X("GW", 512, 1024), X("b1", 0, 512))
+        else:
+            act(X("GW", 512, 1024), X("b1", 0, 512))
+            vts(X("PB", 0, 64), X("b7", 320, 384), -129.0, OP.add)
         gwin = X("GW", 0, WIN)
 
         def gather(buf, lst, o, a, b, eng):
@@ -364,51 +409,25 @@ def rank_program(g, core, T, topo):
 
         def xx(oc, strip, row, side):
             wrap("b7", oc, strip, row, plus=[("idn16", "CK", 64 * side), ("idn", "CK", 128 + 64 * side)])
-        half = 0 if r else 512
-        gather("gl", "KB", 0, half, 1024, act)
-        gather("gr", "KB", 64, half, 1024, act)
-        P_ = X("PI", 0, 64)
-        if r:
-            wrap("b6", 128, "sC2", "cg", plus=[("idn", "ones", 0), ("idn", "ones", 0)])
-            wrap("b6", 192, "sRC", "cg", plus=[("idn16", "CKP", 0), ("idn", "CKP", 64)])
-        else:
-            vcopy(P_, X("b7", 192, 256))
-            vts(X("LFP", 0, 64), P_, 1024, OP.is_ge)
-            vts(X("LF16", 0, 64), P_, 1024, OP.is_ge, 16, OP.mult)
+
+        gather("gl", "KB", 0, 0, 512, act)
+        gather("gr", "KB", 64, 0, 512, act)
         if not last:
-            spread(("b2", "b3"), [(3, "CK", 64), (4, "CK", 192), (2, "LF16", 0)], True, False)
+            for h in range(2):
+                spread1(("b2", "b3"), h, [(1, "CKP", 0), (2, "CKP", 64)], False, False)
+        gather("gl", "KB", 0, 512, 1024, vcopy)
+        gather("gr", "KB", 64, 512, 1024, vcopy)
+        wrap("b4", 0, "sG", "gl", plus=[("idh", "TB", 0), TIE])
+        wrap("b5", 0, "sG", "gr", plus=[("idh", "TB", 64), TIE])
+        gather("gp", "PB", 0, 512, 1024, vcopy)
         if r:
-            def pt(i):
-                return X("pt", 64 * i, 64 * i + 64)
-            vtt(pt(1), X("ee", 0, 64), X("ee", 64, 128), OP.add)
-            vtt(pt(1), pt(0), pt(1), OP.subtract)
-            vtt(pt(2), X("b7", 256, 320), P_, OP.subtract)
-            vtt(pt(2), pt(1), pt(2), OP.mult)
-            vtt(pt(5), P_, pt(2), OP.add)
-            vtt(pt(3), X("b6", 128, 192), X("sd", 0, 64), OP.subtract)
-            vts(pt(4), X("b6", 192, 256), 0.0, OP.is_equal, 4.0, OP.mult)
-            vtt(pt(6), pt(3), pt(4), OP.is_equal)
-            vtt(pt(6), pt(6), X("GPs", 0, 64), OP.mult)
-            vtt(P_, pt(5), pt(6), OP.add)
-        pchunks()
-        if not r:
-            gather("gl", "KB", 0, 0, 512, vcopy)
-            gather("gr", "KB", 64, 0, 512, vcopy)
-        cut = 768 if r else 512
-        gather("gp", "PB", 0, 0, cut, vcopy)
-        gather("gp", "PB", 0, cut, 1024, act)
-        wrap("b4", 0, "sG", "gl", plus=[("id1", "TB", 0)])
-        xx(64, "sL", "gl", 1)
-        xx(192, "sR", "gl", 1)
-        wrap("b5", 0, "sG", "gr", plus=[("id1", "TB", 64)])
-        wrap("b6", 0, "sG", "gp", plus=[("id1", "TB", 128)])
-        if not last:
-            spread(("b2", "b3"), [(1, "CKP", 0), (2, "CKP", 64)], False, False)
-        vts(X("gi", 0, 64), X("ga", 0, 64), 0.375, OP.add)
-        vtt(X("cd", 0, 64), X("gi", 0, 64), X("ga", 0, 64), OP.subtract)
-        vts(X("cc", 0, 64), X("cd", 0, 64), 4.0, OP.mult, 1.0, OP.add)
+            act(X("TB", 128, 192), X("b7", 384, 448), AF.Sign)
+        gather("gp", "PB", 0, 0, 512, act)
         vts(X("tt", 0, 64), X("b4", 0, 64), 1.0, OP.max)
         vtt(X("tt", 64, 128), X("b5", 0, 64), X("tt", 0, 64), OP.max)
+        wrap("b6", 0, "sG", "gp", plus=[("idh", "TB", 128), TIE])
+        xx(64, "sL", "gl", 1)
+        xx(192, "sR", "gl", 1)
         vtt(X("tt", 128, 192), X("b6", 0, 64), X("tt", 64, 128), OP.max)
         vtt(X("rot", 0, 64), X("gi", 0, 64), X("tt", 128, 192), OP.is_ge)
         vtt(X("code", 0, 64), X("rot", 0, 64), X("cc", 0, 64), OP.mult)
@@ -417,66 +436,71 @@ def rank_program(g, core, T, topo):
             dma("S", T.yh[:, I:I + V0], T.OH[:, I:I + V0], [X("OH", I, I + V0)], [])
         else:
             act(X(nxt, I, 2049), X("y1", 0, 1025), AF.Relu, -1.0, 255.0)
+        for h in range(2):
+            spread1(("b2", "b3"), h, [(0, "code", 0)], last, True)
         xx(0, "sL", "gr", 0)
-        spread(("b2", "b3"), [(0, "code", 0)], last, True)
         xx(128, "sR", "gr", 0)
-        wrap("b7", 320, "sR", "gp", plus=[("idn", "nch", 0), ("idn", "nch", 64)])
-        wrap("b7", 256, "sS", "gp", plus=[("idn", "nch", 0), ("idn", "nch", 64)])
+        wrap("b6", 320, "sR", "gp", plus=[("idn16", "k129", 0)] + OWN)
+        wrap("b6", 256, "sS", "gp", plus=[("idn16", "k129", 0), ("idn16", "k129", 0)] + OWN)
         for j, c in enumerate((3, 1, 4, 2)):
             vts(X("MK", 64 * j, 64 * j + 64), X("code", 0, 64), float(c), OP.is_equal)
         act(X("CW", 0, 512), X("b2", 0, 512))
         vcopy(X("CW", 512, 1024), X("b3", 0, 512))
         cwin = X("CW", 0, WIN)
-        vcopy(X("cp", 0, 512), ind(cwin, X("PB", 0, 32)))
-        act(X("cp", 512, 1024), ind(cwin, X("PB", 32, 64)))
+        vcopy(X("cp", 768, 1024), ind(cwin, X("PB", 48, 64)))
+        act(X("cp", 0, 768), ind(cwin, X("PB", 0, 48)))
+        vtt(X("pr", 0, 256), X("b7", 0, 256), X("MK", 0, 256), OP.mult)
         wrap("b5", 0, "sC", "cp", plus=[("idn", "ones", 0)])
         if not last:
             wrap("b4", 0, "sPB", "cp")
             wrap("b4", 64, "sPn", "cp", plus=[("idn16", "CKP", 0), ("idn", "CKP", 64)])
-        vtt(X("pr", 0, 256), X("b7", 0, 256), X("MK", 0, 256), OP.mult)
-        vts(X("sd", 0, 64), X("b7", 320, 384), 0.0, OP.is_equal, 2.0, OP.mult)
         vtt(X("xs", 0, 128), X("pr", 0, 128), X("pr", 128, 256), OP.add)
+        vtt(X("K1", 0, 128), X("KF", 0, 128), X("xs", 0, 128), OP.add)
+        vts(X("sd", 0, 64), X("b6", 320, 384), 0.0, OP.is_equal, 2.0, OP.mult)
         vts(X("sd", 64, 128), X("sd", 0, 64), 1.0, OP.add)
-        vtt(X("K1", 0, 128), X("KI", 0, 128), X("xs", 0, 128), OP.add)
-        vtt(X("dS", 0, 64), X("b7", 256, 320), X("K1", 0, 64), OP.subtract)
-        vtt(X("dS", 64, 128), X("b7", 256, 320), X("K1", 64, 128), OP.subtract)
+        vtt(X("dS", 0, 64), X("b6", 256, 320), X("KF", 0, 64), OP.subtract)
+        vtt(X("dS", 64, 128), X("b6", 256, 320), X("KF", 64, 128), OP.subtract)
         vtt(X("ee", 0, 64), X("b5", 0, 64), X("sd", 0, 64), OP.is_equal)
         vtt(X("ee", 64, 128), X("b5", 0, 64), X("sd", 64, 128), OP.is_equal)
         vtt(X("te", 0, 128), X("ee", 0, 128), X("dS", 0, 128), OP.mult)
-        vtt(X("KI", 0, 128), X("K1", 0, 128), X("te", 0, 128), OP.add)
-        vcopy(X("KU", 0, 128), X("KI", 0, 128))
-        act(X("rr", 0, 672), ind(win, X("KU", 64, 106)))
-        if last:
-            vts(X("CI", 0, 128), X("KI", 0, 128), 15, OP.bitwise_and)
-            vtt(X("fh", 0, 128), X("KI", 0, 128), X("CI", 0, 128), OP.subtract)
-            vcopy(X("fl", 0, 128), X("CI", 0, 128))
-        vcopy(X("rr", 672, 1024), ind(win, X("KU", 106, 128)))
         if not last:
-            vts(X("pt", 0, 64), X("b5", 0, 64), 0.0, OP.is_ge)
-            vcopy(X("PPu", 0, 64), X("b4", 0, 64))
-            vcopy(X("GPs", 0, 64), X("b4", 64, 128))
+            vts(X("PPu", 0, 64), X("b4", 0, 64), -129.0, OP.add)
+            act(X("sib", 0, 64), X("b6", 256, 320))
+            act(X("GPs", 0, 64), X("b4", 64, 128))
+            act(X("sp", 0, 64), X("b5", 0, 64), AF.Sign, 1.0, 0.5)
+            act(pt(0), X("sp", 0, 64), AF.Relu)
+        vtt(X("KF", 0, 128), X("K1", 0, 128), X("te", 0, 128), OP.add)
+        vcopy(X("KU", 0, 128), X("KF", 0, 128))
+        if last:
+            act(X("fh", 0, 128), X("KF", 0, 128))
+            vtt(X("fl", 0, 128), X("KF", 0, 128), X("fh", 0, 128), OP.subtract)
+        act(X("rr", 0, 320), ind(win, X("KU", 64, 84)))
+        act(X("rr", 320, 640), ind(win, X("KU", 84, 104)))
+        vcopy(X("rr", 640, 1024), ind(win, X("KU", 104, 128)))
+        if not last:
+            chunks()
             act(X("cg", 0, 512), ind(cwin, X("PPu", 0, 32)))
+            act(X("CK", 128, 256), X("b4", 128, 256), scale=1.0, bias=2064.0)
+            act(X("cg", 512, 1024), ind(cwin, X("PPu", 32, 64)))
         dst = "OH" if last else nxt
-        vtt(X(dst, 672, 1024), ind(win, X("KU", 42, 64)), X("rr", 672, 1024), OP.max)
-        if last:
-            dma("S", T.yh[:, 672:1024], T.OH[:, 672:1024], [X("OH", 672, 1024)], [])
-        vtt(X(dst, 0, 672), ind(win, X("KU", 0, 42)), X("rr", 0, 672), OP.max)
-        if last:
-            dma("S", T.yh[:, 0:672], T.OH[:, 0:672], [X("OH", 0, 672)], [])
+        for a, b in ((640, 1024), (0, 320), (320, 640)):
+            vtt(X(dst, a, b), ind(win, X("KU", a // 16, b // 16)), X("rr", a, b), OP.max)
+            if last:
+                dma("S", T.yh[:, a:b], T.OH[:, a:b], [X("OH", a, b)], [])
         cur, nxt = nxt, cur
 
-    for h in range(2):
+    for b in range(4):
+        bank = "b%d" % b
+        o = X("OK", 512 * b, 512 * b + 512)
         fns = []
-        for j, (part, buf) in enumerate(((0, "fh"), (0, "fl"), (1, "fh"), (1, "fl"))):
+        for j, buf in enumerate(("fh", "fl")):
             for k in range(16):
-                c = 64 * part + 32 * h
-                fns.append(mm(T["b%d" % h][:, k:512:16], T.ES[:, 144 * k + 16 - part:144 * k + 144 - part], T[buf][:, c:c + 32],
-                              j == 0 and k == 0, j == 3 and k == 15))
-        emit("P", fns, [X("ES", 0, 2304), X("fh", 0, 128), X("fl", 0, 128)], [X("b%d" % h, 0, 512)])
-        act(X("OK", 512 * h, 512 * h + 512), X("b%d" % h, 0, 512))
-        for a in range(2):
-            dma("A", T.yk[:, 1024 * a + 512 * h:1024 * a + 512 * h + 512], T.OK[a::16, 512 * h:512 * h + 512],
-                [X("OK", 512 * h, 512 * h + 512)], [])
-    cnt["sent"] = nsent
+                fns.append(mm(T[bank][0:8, k:512:16], T.idp[:, 8 * k:8 * k + 8], T[buf][:, 32 * b:32 * b + 32],
+                              j == 0 and k == 0, j == 1 and k == 15))
+        emit("P", fns, [X("idp", 0, 128), X("fh", 0, 128), X("fl", 0, 128)], [X(bank, 0, 512)])
+        emit("A", [lambda: g.scalar.activation(T.OK[0:8, 512 * b:512 * b + 512], T[bank][0:8, 0:512], AF.Copy)],
+             [X(bank, 0, 512)], [o])
+        dma("S", T.yk[:, 512 * b:512 * b + 512], T.OK[0:8, 512 * b:512 * b + 512], [o], [])
+    cnt["sent"] = nsent[0]
     for s, c in cnt.items():
         g.wait_ge(T.sem[s], c)

from concourse.bass import DstId, RemoteDMATransfer
from concourse.mybir import AluOpType, ActivationFunctionType

OP = AluOpType
AF = ActivationFunctionType
I, V0, GH, RO = 1024, 353, 96, 3
LEAF = WIN = 2176

SCRATCH = {"b%d" % _b: ("psum", [128, 512], "float32") for _b in range(8)}
for _dt, _names in (
        ("int32", "hl 360 hi 1024 vi 360 si 48 pi 8 pq 8 KI 128 gi 64"),
        ("uint16", "su 48 KU 128 KB 128 PB 64 PPu 64"),
        ("bfloat16", "HA 2064 HB 2064 vo 368 sh 672 sv 672 lh 672 lv 672 hcl 2176 hcr 2176 hr2 1024 mm 3072 zz 1024 rl 1024 rr 1024 "
                     "GW 2176 CW 2176 gl 1024 gr 1024 gp 1024 cp 1024 cg 1024 ones 144 ec 144 ES 2304 bc 16 BS 144 BSn 144 sG 144 sL 144 "
                     "sR 144 sS 144 sC 144 sC2 144 sPn 144 sPB 144 sRC 144 sO 144 id1 128 idn 128 idn16 128 id16 128 id64 128 id512 128 "
                     "idnb 128 idh 128 idp 128 PW 2064 nrow 1024 chi 64 k129 64 sgn 128 CK 256 "
                     "TB 192 CKP 128 ghi 64 glo 64 code 64 fh 128 fl 128 nch 128 cq 256"),
        ("float32", "y1 1032 id32 128 qf 8 jr 16 oh 16 ww 16 c16 64 KF 128 PI 64 GPs 64 sib 64 sp 64 "
                    "q1s 128 qm 128 qq 128 ga 64 cd 64 cc 64 tt 192 rot 64 MK 256 pr 256 xs 128 K1 128 dS 128 sd 128 ee 128 te 128 "
                    "pt 512 OK 2048 OH 1384")):
    _w = _names.split()
    for _n, _c in zip(_w[::2], _w[1::2]):
        SCRATCH[_n] = ("sbuf", [128, int(_c)], _dt)
SEMAPHORES = ["V", "A", "P", "G", "arrH", "arrV", "sent"] + ["d%d" % _i for _i in range(16)]


def sends(T, topo, q):
    src = T.cores[q]
    dst = {d: T.cores[(q + d) % 8] for d in range(1, 8)}
    near = [d for d in dst if topo.chip(dst[d]) == topo.chip(src)]
    far = [d for d in dst if d not in near]
    pool = list(topo.engines(src, dst[far[0]]))

    def direct(d):
        a, b = topo.chip(src), topo.chip(dst[d])
        return topo.mates(a, b) or topo.same_plane(a, b)
    far.sort(key=lambda d: (direct(d), d))
    out = {}
    spare = len(pool) - len(far)
    used = 0
    for d in far:
        k = 2 if spare > 0 else 1
        spare -= k - 1
        out[d] = pool[used:used + k]
        used += k
    rest = [e for e in topo.engines(src, dst[near[0]]) if e not in pool]
    for j, d in enumerate(near):
        out[d] = rest[j:j + 1]
    return out


def rank_program(g, core, T, topo):
    rank = T.rank_of(core)
    if rank is None:
        return
    queue = {"V": g.vector, "A": g.scalar, "P": g.tensor, "G": g, "S": g.sync}
    cnt = {}
    known = {q: {} for q in queue}
    acc = {}
    ndma = [0]

    def psum(name):
        return name[0] == "b" and name[1:].isdigit()

    def hazards(q, rd, wr):
        deps = []
        for ops, w in ((rd, False), (wr, True)):
            for _, name, a, b in ops:
                if psum(name):
                    deps += [r for qq, r in acc.setdefault(name, {}).items() if qq != q]
                    continue
                for k, x, y, r in acc.setdefault(name, []):
                    if x < b and y > a and (w or k) and not (r[2] == q and (q == "P" or not k)):
                        deps.append(r)
        return deps

    def note(q, rd, wr, rec):
        for ops, w in ((rd, False), (wr, True)):
            for _, name, a, b in ops:
                if psum(name):
                    acc[name][q] = rec
                    continue
                lst = acc[name]
                if w:
                    lst[:] = [t for t in lst if not (t[1] >= a and t[2] <= b)]
                else:
                    lst[:] = [t for t in lst if t[0] or t[3][2] != rec[2] or not (t[1] >= a and t[2] <= b)]
                lst.append((w, a, b, rec))

    def sync(q, deps):
        kn = known[q]
        best = {}
        for r in deps:
            if kn.get(r[0], 0) < r[1] and (r[0] not in best or best[r[0]][1] < r[1]):
                best[r[0]] = r
        for r in sorted(best.values(), key=lambda r: -len(r[3])):
            if kn.get(r[0], 0) >= r[1]:
                continue
            queue[q].wait_ge(T.sem[r[0]], r[1])
            for s, c in r[3].items():
                kn[s] = max(kn.get(s, 0), c)
            kn[r[0]] = r[1]

    def emit(q, fns, rd, wr):
        sync(q, hazards(q, rd, wr))
        for f in fns:
            f().then_inc(T.sem[q], 1)
            cnt[q] = cnt.get(q, 0) + 1
        note(q, rd, wr, (q, cnt[q], q, dict(known[q])))

    def dma(q, out, in_, rd, wr):
        sync(q, hazards(q, rd, wr))
        s = "d%d" % ndma[0]
        ndma[0] += 1
        cnt[s] = 16
        queue[q].dma_start(out, in_).then_inc(T.sem[s], 16)
        note("D", rd, wr, (s, 16, "D", dict(known[q])))

    def X(name, a, b, step=1):
        return (T[name][:, a:b] if step == 1 else T[name][:, a:b:step], name, a, b)

    def ind(win, off):
        return (win[0].indirect(off[0]), win, off)

    def flat(*ops):
        out = []
        for o in ops:
            out += [o[1], o[2]] if len(o) == 3 else [o]
        return out

    def vcopy(out, in_):
        if len(out) == 3:
            emit("V", [lambda: g.vector.tensor_copy(out[0], in_[0])], [in_, out[2]], [out[1]])
        else:
            emit("V", [lambda: g.vector.tensor_copy(out[0], in_[0])], flat(in_), [out])

    def vtt(out, a, b, op):
        emit("V", [lambda: g.vector.tensor_tensor(out[0], a[0], b[0], op)], flat(a, b), [out])

    def vts(out, a, s1, op0, s2=None, op1=None):
        rd = [a] + [s for s in (s1, s2) if isinstance(s, tuple)]
        v1 = s1[0] if isinstance(s1, tuple) else s1
        v2 = s2[0] if isinstance(s2, tuple) else s2
        if op1 is None:
            emit("V", [lambda: g.vector.tensor_scalar(out[0], a[0], v1, None, op0)], rd, [out])
        else:
            emit("V", [lambda: g.vector.tensor_scalar(out[0], a[0], v1, v2, op0, op1)], rd, [out])

    def vset(out, c):
        emit("V", [lambda: g.vector.memset(out[0], c)], [], [out])

    def act(out, in_, func=AF.Copy, scale=None, bias=None):
        kw = {}
        rd = flat(in_)
        for key, v in (("scale", scale), ("bias", bias)):
            if v is not None:
                kw[key] = v[0] if isinstance(v, tuple) else v
                rd = rd + ([v] if isinstance(v, tuple) else [])
        emit("A", [lambda: g.scalar.activation(out[0], in_[0], func, **kw)], rd, [out])

    def gsel(out, in_, pattern, op, base, cm):
        emit("G", [lambda: g.affine_select(out[0], in_[0], pattern, op, 0.0, base, cm)], [in_], [out])

    def giota(out, pattern, base, cm, flag):
        kw = {"allow_small_or_imprecise_dtypes": True} if flag else {}
        emit("G", [lambda: g.iota(out[0], pattern, base, cm, **kw)], [], [out])

    def mm(out, lhsT, rhs, start, stop):
        return lambda: g.tensor.matmul(out, lhsT, rhs, start, stop)

    def wrap(bank, oc, strip, row, off=0, first=True, last=True, plus=()):
        fns = []
        rd = [X(strip, 0, 144), X(row, off, off + 1024)]
        for j, (idm, buf, a) in enumerate(plus):
            fns.append(mm(T[bank][:, oc:oc + 64], T[idm][:, 0:128], T[buf][:, a:a + 64], first and j == 0, False))
            rd += [X(idm, 0, 128), X(buf, a, a + 64)]
        for k in range(16):
            fns.append(mm(T[bank][:, oc:oc + 64], T[strip][:, 16 - k:144 - k], T[row][:, off + k:off + 1024:16],
                          first and not plus and k == 0, last and k == 15))
        emit("P", fns, rd, [X(bank, oc, oc + 64)])

    def full(bank, oc, terms, n, last=True, first=True):
        fns = []
        rd = []
        for j, (idm, buf, a) in enumerate(terms):
            fns.append(mm(T[bank][:, oc:oc + n], T[idm][:, 0:128], T[buf][:, a:a + n], first and j == 0, last and j == len(terms) - 1))
            rd += [X(idm, 0, 128), X(buf, a, a + n)]
        emit("P", fns, rd, [X(bank, oc, oc + n)])

    def spread1(banks, h, parts, first, last):
        fns = []
        rd = [X("ES", 0, 2304)]
        for j, (part, buf, col) in enumerate(parts):
            for k in range(8 * h, 8 * h + 8):
                fns.append(mm(T[banks[h]][:, 64 * (k % 8):64 * (k % 8) + 64], T.ES[:, 144 * k + 16 - part:144 * k + 144 - part],
                              T[buf][:, col:col + 64], first and j == 0 and k % 8 == 0,
                              last and j == len(parts) - 1 and k % 8 == 7))
            rd.append(X(buf, col, col + 64))
        emit("P", fns, rd, [X(banks[h], 0, 512)])

    dma("S", T.hl[:, 0:V0], T.h0[:, I:I + V0], [], [X("hl", 0, V0)])
    dma("A", T.si[:, 0:42], T.sl[:, :], [], [X("si", 0, 42)])
    dma("S", T.KI[:, 0:64], T.kl[:, :], [], [X("KI", 0, 64)])
    dma("A", T.KI[:, 64:128], T.kr[:, :], [], [X("KI", 64, 128)])
    dma("S", T.vi[:, 0:V0], T.vel[:, :], [], [X("vi", 0, V0)])
    dma("S", T.hi[:, :], T.h0[:, 0:I], [], [X("hi", 0, 1024)])

    vset(X("ones", 0, 144), 1.0)
    giota(X("pi", 0, 1), [[0, 1]], 0, 1, False)
    giota(X("jr", 0, 16), [[1, 16]], 0, 0, True)
    gsel(X("ec", 0, 144), X("ones", 0, 144), [[-1, 16], [-16, 9]], OP.is_equal, 16, 1)
    gsel(X("bc", 0, 9), X("ones", 0, 9), [[-16, 9]], OP.is_ge, 16, 1)
    gsel(X("bc", 0, 9), X("bc", 0, 9), [[16, 9]], OP.is_ge, -1, -1)
    gsel(X("id1", 0, 128), X("ones", 0, 128), [[-1, 128]], OP.is_equal, 0, 1)
    giota(X("c16", 0, 64), [[16, 64]], 0, 0, True)
    giota(X("chi", 0, 64), [[1, 64]], 129, 0, True)
    vset(X("BS", 0, 144), 0.0)
    vset(X("ES", 0, 2304), 0.0)
    vts(X("pq", 0, 1), X("pi", 0, 1), 15, OP.bitwise_and)
    vcopy(X("qf", 0, 1), X("pq", 0, 1))
    vts(X("oh", 0, 16), X("jr", 0, 16), X("qf", 0, 1), OP.is_equal)
    vcopy(X("BS", 0, 144, 16), X("bc", 0, 9))
    vcopy(X("ES", 0, 2304, 16), X("ec", 0, 144))
    vcopy(X("HA", I, I + V0), X("hl", 0, V0))
    vcopy(X("su", 0, 42), X("si", 0, 42))
    act(X("nch", 64, 128), X("c16", 0, 64), AF.Identity, 0.0, X("qf", 0, 1))
    act(X("sh", 0, 672), ind(X("HA", I, I + V0), X("su", 0, 42)))
    vcopy(X("KU", 0, 128), X("KI", 0, 128))
    vcopy(X("vo", 0, V0), X("vi", 0, V0))
    vts(X("ww", 11, 12), X("oh", 0, 1), 256.0, OP.mult)
    vts(X("ww", 9, 10), X("oh", 1, 2), 16.0, OP.mult, X("ww", 11, 12), OP.add)

    mine = sends(T, topo, rank)
    nsent = [0]

    def exchange(buf, land, sem):
        sync("G", hazards("G", [X(buf, 0, 672)], []))
        tr = []
        for d in range(1, 8):
            rid, pid, _ = topo.addr(T.cores[(rank + d) % 8])
            tr.append(RemoteDMATransfer(src=T[buf][:, GH * (d - 1):GH * d], dst=T[land][:, GH * (d - 1):GH * d],
                                        dst_ids=[DstId(rid=rid, pnc=pid)], dma_engine_mask=sum(1 << e for e in mine[d]),
                                        remote_sem=T.sem[sem]))
            nsent[0] += len(mine[d])
        g.remote_dma_fused(tr, local_sem=T.sem.sent)
    exchange("sh", "lh", "arrH")

    act(X("PW", 0, 1024), X("ES", 0, 1024), AF.Identity, 0.0, X("ww", 9, 10))
    for h in range(2):
        fns = []
        for part, buf, col in ((0, "chi", 0), (1, "nch", 64)):
            for k in range(16):
                c = col + 32 * h
                fns.append(mm(T["b%d" % h][:, k:512:16], T.ES[:, 144 * k + 16 - part:144 * k + 144 - part], T[buf][:, c:c + 32],
                              part == 0 and k == 0, part == 1 and k == 15))
        emit("P", fns, [X("ES", 0, 2304), X("chi", 0, 64), X("nch", 64, 128)], [X("b%d" % h, 0, 512)])
    act(X("nrow", 0, 512), X("b0", 0, 512))
    act(X("nrow", 512, 1024), X("b1", 0, 512))
    act(X("sv", 0, 672), ind(X("vo", 0, V0), X("su", 0, 42)))
    exchange("sv", "lv", "arrV")
    narr = sum(len(sends(T, topo, (rank - d) % 8)[d]) for d in range(1, 8))
    for land, sem in (("lh", "arrH"), ("lv", "arrV")):
        cnt[sem] = narr
        acc.setdefault(land, []).append((True, 0, 672, (sem, narr, "R", {})))

    def scatter(a):
        vcopy(ind(X("PW", 0, 2049), X("KU", a, a + 64)), X("nrow", 0, 1024))

    vts(X("ww", 10, 11), X("oh", 1, 2), 129.0, OP.mult)
    for j, a, w, b in ((0, ("oh", 0), 1.0, ("oh", 1)), (1, ("oh", 2), 16.0, ("oh", 3)), (2, ("oh", 4), 16.0, ("oh", 5)),
                       (3, ("ww", 1), 1.0, ("ww", 2)), (4, ("oh", 1), 16.0, ("oh", 2)), (5, ("oh", 2), 64.0, ("oh", 1)),
                       (6, ("oh", 3), 16.0, ("oh", 4)), (7, ("oh", 0), 1.0, ("oh", 0)), (8, ("oh", 2), 16.0, ("ww", 10))):
        vts(X("ww", j, j + 1), X(a[0], a[1], a[1] + 1), w, OP.mult, X(b[0], b[1], b[1] + 1), OP.add)
    vcopy(X("KF", 0, 128), X("KI", 0, 128))
    vcopy(X("HA", 0, I), X("hi", 0, I))
    for nm, w in (("idn", -1.0), ("idn16", -16.0), ("id64", 64.0), ("id32", 1.0), ("id512", 512.0), ("idnb", -4096.0),
                  ("idh", 0.5), ("id16", 16.0)):
        act(X(nm, 0, 128), X("id1", 0, 128), scale=w)
    act(X("nch", 0, 64), X("c16", 0, 64))
    gsel(X("idp", 0, 128), X("ones", 0, 128), [[-1, 16], [-16, 8]], OP.is_equal, 0, 1)
    for nm in ("hcl", "hcr", "GW"):
        giota(X(nm, 1024, LEAF), [[0, LEAF - 1024]], 0, 0, True)
    act(X("BSn", 0, 144), X("BS", 0, 144), scale=-1.0)
    for j, c in enumerate((0.0, 0.5, 0.25, 0.75)):
        vset(X("cq", 64 * j, 64 * j + 64), c)
    vset(X("k129", 0, 64), 129.0)
    for nm, w in (("sG", ("ww", 0)), ("sL", ("ww", 1)), ("sR", ("ww", 2)), ("sS", ("ww", 3)), ("sC", ("oh", 0)), ("sO", ("oh", 1)),
                  ("sC2", ("ww", 7)), ("sPn", ("ww", 4)), ("sPB", ("ww", 5)), ("sRC", ("ww", 6))):
        act(X(nm, 0, 144), X("BS", 0, 144), scale=X(w[0], w[1], w[1] + 1))

    P_ = X("PI", 0, 64)
    OWN = [("idn", "nch", 0), ("idn", "nch", 64)]
    TIE = ("idh", "ones", 0)

    def pt(i):
        return X("pt", 64 * i, 64 * i + 64)

    def chunks():
        vts(X("CK", 0, 128), X("KF", 0, 128), 0.0625, OP.mult, 128.53125, OP.add)
        full("b4", 128, [("id32", "KF", 0), ("idn16", "CK", 0)], 128)
        full("b4", 256, [("id32", "KF", 0)] + OWN, 64)
        full("b4", 320, [("id32", "KF", 64)] + OWN, 64)
        for h in range(2):
            spread1(("b0", "b1"), h, [(2, "CK", 0), (4, "CK", 64)], True, False)

    scatter(0)
    chunks()
    act(X("CK", 128, 256), X("b4", 128, 256), scale=1.0, bias=2064.0)
    act(X("CW", 1024, LEAF), X("ES", 0, LEAF - 1024), AF.Identity, 0.0, X("ww", 8, 9))
    scatter(64)
    wrap("b6", 128, "sC", "PW")
    wrap("b6", 192, "sO", "PW")
    vcopy(X("CKP", 0, 128), X("b6", 128, 256))
    full("b6", 0, [("id16", "CKP", 0), ("id1", "CKP", 64)], 64)
    full("b6", 64, [("id1", "CKP", 0), ("id64", "CKP", 64)], 64)
    full("b6", 384, [("id16", "CKP", 0), ("id1", "CKP", 64), ("idn16", "k129", 0)] + OWN, 64)
    vts(X("PB", 0, 64), X("b6", 64, 128), -129.0, OP.add)
    act(P_, X("b6", 0, 64), scale=1.0, bias=-2064.0)
    act(X("TB", 128, 192), X("b6", 384, 448), AF.Sign)
    vcopy(X("HA", I + V0, 2049), X("lh", 0, 672))

    cur, nxt = "HA", "HB"
    for r in range(RO):
        last = r == RO - 1
        win = X(cur, 0, 2049)
        wl, wr = X("hcl", 0, 2049), X("hcr", 0, 2049)
        act(X("hcl", 0, 1024), ind(win, X("KU", 0, 64)))
        vcopy(X("hcr", 0, 1024), ind(win, X("KU", 64, 128)))
        act(X("sgn", 0, 128), X("CK", 0, 128), AF.Sign, 1.0, -192.5)
        act(X("TB", 0, 128), X("b4", 256, 384), AF.Sign)
        for h in range(2):
            spread1(("b0", "b1"), h, [(3, "CK", 128), (5, "CK", 192)], False, False)
        if r:
            wrap("b7", 128, "sC2", "cg", plus=[("idn", "ones", 0), ("idn", "ones", 0)])
            wrap("b7", 192, "sRC", "cg", plus=[("idn16", "CKP", 0), ("idn", "CKP", 64)])
        wrap("b4", 0, "BS", "hcl", 0, True, False)
        full("b6", 0, [("idn", "cq", 128)], 128, False)
        wrap("b6", 64, "BSn", "hcl", 0, False, False)
        wrap("b4", 64, "BS", "hcr", 0, False, False)
        full("b4", 0, [("idnb", "sgn", 0), ("idnb", "ones", 0)], 128, True, False)
        full("b7", 0, [("id1", "CK", 0), ("id64", "CK", 128), ("id512", "sgn", 0)], 128)
        act(X("zz", 0, 512), ind(wl, X("KU", 64, 96)))
        act(X("zz", 512, 1024), ind(wl, X("KU", 96, 128)))
        vtt(X("mm", 1024, 2048), ind(wr, X("KU", 64, 128)), X("hcl", 0, 1024), OP.max)
        full("b2", 0, [("idn", "hcl", 0), ("id1", "zz", 0)], 512)
        full("b3", 0, [("idn", "hcl", 512), ("id1", "zz", 512)], 512)
        act(X("hr2", 0, 1024), X("hcr", 0, 1024))
        act(X("rl", 0, 512), X("b2", 0, 512), AF.Relu)
        act(X("rl", 512, 1024), X("b3", 0, 512), AF.Relu)
        full("b5", 0, [("idn", "cq", 0)], 128, False)
        vtt(X("mm", 2048, 3072), ind(wl, X("KU", 0, 64)), X("hcr", 0, 1024), OP.max)
        wrap("b5", 64, "BSn", "mm", 1024, False, False)
        wrap("b6", 64, "BSn", "rl", 0, False, False)
        vtt(X("mm", 0, 1024), ind(wr, X("KU", 0, 64)), X("hr2", 0, 1024), OP.max)
        wrap("b6", 0, "BSn", "mm", 2048, False, True)
        act(X("q1s", 0, 128), X("b6", 0, 128))
        wrap("b5", 0, "BSn", "mm", 0, False, True)
        full("b2", 0, [("id1", cur, I), ("id1", "vo", 0)], V0)
        act(X("y1", 0, V0), X("b2", 0, V0), AF.Relu, -1.0, 255.0)
        if not last:
            full("b3", 0, [("id1", cur, I + V0), ("id1", "lv", 0)], 336)
            full("b6", 128, [("id1", cur, I + V0 + 336), ("id1", "lv", 336)], 336)
            act(X("y1", V0, V0 + 336), X("b3", 0, 336), AF.Relu, -1.0, 255.0)
            act(X("y1", V0 + 336, 1025), X("b6", 128, 464), AF.Relu, -1.0, 255.0)
        vts(X("KB", 0, 128), X("b7", 0, 128), 383.0, OP.add)
        if r:
            vtt(pt(1), X("ee", 0, 64), X("ee", 64, 128), OP.add)
            vtt(pt(3), X("b7", 128, 192), X("sd", 0, 64), OP.subtract)
            vts(pt(4), X("b7", 192, 256), 0.0, OP.is_equal, 4.0, OP.mult)
            vtt(pt(2), X("sib", 0, 64), P_, OP.subtract)
            vtt(pt(1), pt(0), pt(1), OP.subtract)
            vtt(pt(6), pt(3), pt(4), OP.is_equal)
        vtt(X("qm", 0, 128), X("q1s", 0, 128), X("b5", 0, 128), OP.max)
        vtt(X("qq", 0, 128), X("b4", 0, 128), X("qm", 0, 128), OP.add)
        vtt(X("ghi", 0, 64), X("qq", 0, 64), X("qq", 64, 128), OP.max)
        vtt(X("ga", 0, 64), X("qq", 0, 64), X("qq", 64, 128), OP.max)
        vtt(X("glo", 0, 64), X("ga", 0, 64), X("ghi", 0, 64), OP.subtract)
        for part, buf in ((0, "ghi"), (1, "glo")):
            for h in range(2):
                spread1(("b0", "b1"), h, [(part, buf, 0)], False, part == 1)
        if not last:
            spread1(("b2", "b3"), 0, [(3, "CK", 64), (4, "CK", 192)], True, False)
        if r:
            vtt(pt(2), pt(1), pt(2), OP.mult)
            vtt(pt(6), pt(6), X("GPs", 0, 64), OP.mult)
            vtt(pt(5), P_, pt(2), OP.add)
            vtt(P_, pt(5), pt(6), OP.add)
            vts(X("CKP", 0, 64), P_, 0.0625, OP.mult, 128.53125, OP.add)
            full("b7", 320, [("id32", "PI", 0), ("idn16", "CKP", 0)], 64)
            full("b7", 384, [("id32", "PI", 0)] + OWN, 64)
        vts(X("gi", 0, 64), X("ga", 0, 64), 0.375, OP.add)
        vtt(X("cd", 0, 64), X("gi", 0, 64), X("ga", 0, 64), OP.subtract)
        if not last:
            spread1(("b2", "b3"), 1, [(3, "CK", 64), (4, "CK", 192)], True, False)
        if r:
            vts(X("CKP", 64, 128), X("b7", 320, 384), 2064.0, OP.add)
            full("b7", 320, [("id1", "CKP", 0), ("id64", "CKP", 64)], 64)
        vts(X("cc", 0, 64), X("cd", 0, 64), 4.0, OP.mult, 1.0, OP.add)
        act(X("GW", 0, 512), X("b0", 0, 512))
        if not r:
            vcopy(X("GW", 512, 1024), X("b1", 0, 512))
        else:
            act(X("GW", 512, 1024), X("b1", 0, 512))
            vts(X("PB", 0, 64), X("b7", 320, 384), -129.0, OP.add)
        gwin = X("GW", 0, WIN)

        def gather(buf, lst, o, a, b, eng):
            eng(X(buf, a, b), ind(gwin, X(lst, o + a // 16, o + b // 16)))

        def xx(oc, strip, row, side):
            wrap("b7", oc, strip, row, plus=[("idn16", "CK", 64 * side), ("idn", "CK", 128 + 64 * side)])

        gather("gl", "KB", 0, 0, 512, act)
        gather("gr", "KB", 64, 0, 512, act)
        if not last:
            for h in range(2):
                spread1(("b2", "b3"), h, [(1, "CKP", 0), (2, "CKP", 64)], False, False)
        gather("gl", "KB", 0, 512, 1024, vcopy)
        gather("gr", "KB", 64, 512, 1024, vcopy)
        wrap("b4", 0, "sG", "gl", plus=[("idh", "TB", 0), TIE])
        wrap("b5", 0, "sG", "gr", plus=[("idh", "TB", 64), TIE])
        gather("gp", "PB", 0, 512, 1024, vcopy)
        if r:
            act(X("TB", 128, 192), X("b7", 384, 448), AF.Sign)
        gather("gp", "PB", 0, 0, 512, act)
        vts(X("tt", 0, 64), X("b4", 0, 64), 1.0, OP.max)
        vtt(X("tt", 64, 128), X("b5", 0, 64), X("tt", 0, 64), OP.max)
        wrap("b6", 0, "sG", "gp", plus=[("idh", "TB", 128), TIE])
        xx(64, "sL", "gl", 1)
        xx(192, "sR", "gl", 1)
        vtt(X("tt", 128, 192), X("b6", 0, 64), X("tt", 64, 128), OP.max)
        vtt(X("rot", 0, 64), X("gi", 0, 64), X("tt", 128, 192), OP.is_ge)
        vtt(X("code", 0, 64), X("rot", 0, 64), X("cc", 0, 64), OP.mult)
        if last:
            act(X("OH", I, I + V0), X("y1", 0, V0), AF.Relu, -1.0, 255.0)
            dma("S", T.yh[:, I:I + V0], T.OH[:, I:I + V0], [X("OH", I, I + V0)], [])
        else:
            act(X(nxt, I, 2049), X("y1", 0, 1025), AF.Relu, -1.0, 255.0)
        for h in range(2):
            spread1(("b2", "b3"), h, [(0, "code", 0)], last, True)
        xx(0, "sL", "gr", 0)
        xx(128, "sR", "gr", 0)
        wrap("b6", 320, "sR", "gp", plus=[("idn16", "k129", 0)] + OWN)
        wrap("b6", 256, "sS", "gp", plus=[("idn16", "k129", 0), ("idn16", "k129", 0)] + OWN)
        for j, c in enumerate((3, 1, 4, 2)):
            vts(X("MK", 64 * j, 64 * j + 64), X("code", 0, 64), float(c), OP.is_equal)
        act(X("CW", 0, 512), X("b2", 0, 512))
        vcopy(X("CW", 512, 1024), X("b3", 0, 512))
        cwin = X("CW", 0, WIN)
        vcopy(X("cp", 768, 1024), ind(cwin, X("PB", 48, 64)))
        act(X("cp", 0, 768), ind(cwin, X("PB", 0, 48)))
        vtt(X("pr", 0, 256), X("b7", 0, 256), X("MK", 0, 256), OP.mult)
        wrap("b5", 0, "sC", "cp", plus=[("idn", "ones", 0)])
        if not last:
            wrap("b4", 0, "sPB", "cp")
            wrap("b4", 64, "sPn", "cp", plus=[("idn16", "CKP", 0), ("idn", "CKP", 64)])
        vtt(X("xs", 0, 128), X("pr", 0, 128), X("pr", 128, 256), OP.add)
        vtt(X("K1", 0, 128), X("KF", 0, 128), X("xs", 0, 128), OP.add)
        vts(X("sd", 0, 64), X("b6", 320, 384), 0.0, OP.is_equal, 2.0, OP.mult)
        vts(X("sd", 64, 128), X("sd", 0, 64), 1.0, OP.add)
        vtt(X("dS", 0, 64), X("b6", 256, 320), X("KF", 0, 64), OP.subtract)
        vtt(X("dS", 64, 128), X("b6", 256, 320), X("KF", 64, 128), OP.subtract)
        vtt(X("ee", 0, 64), X("b5", 0, 64), X("sd", 0, 64), OP.is_equal)
        vtt(X("ee", 64, 128), X("b5", 0, 64), X("sd", 64, 128), OP.is_equal)
        vtt(X("te", 0, 128), X("ee", 0, 128), X("dS", 0, 128), OP.mult)
        if not last:
            vts(X("PPu", 0, 64), X("b4", 0, 64), -129.0, OP.add)
            act(X("sib", 0, 64), X("b6", 256, 320))
            act(X("GPs", 0, 64), X("b4", 64, 128))
            act(X("sp", 0, 64), X("b5", 0, 64), AF.Sign, 1.0, 0.5)
            act(pt(0), X("sp", 0, 64), AF.Relu)
        vtt(X("KF", 0, 128), X("K1", 0, 128), X("te", 0, 128), OP.add)
        vcopy(X("KU", 0, 128), X("KF", 0, 128))
        if last:
            act(X("fh", 0, 128), X("KF", 0, 128))
            vtt(X("fl", 0, 128), X("KF", 0, 128), X("fh", 0, 128), OP.subtract)
        act(X("rr", 0, 320), ind(win, X("KU", 64, 84)))
        act(X("rr", 320, 640), ind(win, X("KU", 84, 104)))
        vcopy(X("rr", 640, 1024), ind(win, X("KU", 104, 128)))
        if not last:
            chunks()
            act(X("cg", 0, 512), ind(cwin, X("PPu", 0, 32)))
            act(X("CK", 128, 256), X("b4", 128, 256), scale=1.0, bias=2064.0)
            act(X("cg", 512, 1024), ind(cwin, X("PPu", 32, 64)))
        dst = "OH" if last else nxt
        for a, b in ((640, 1024), (0, 320), (320, 640)):
            vtt(X(dst, a, b), ind(win, X("KU", a // 16, b // 16)), X("rr", a, b), OP.max)
            if last:
                dma("S", T.yh[:, a:b], T.OH[:, a:b], [X("OH", a, b)], [])
        cur, nxt = nxt, cur

    for b in range(4):
        bank = "b%d" % b
        o = X("OK", 512 * b, 512 * b + 512)
        fns = []
        for j, buf in enumerate(("fh", "fl")):
            for k in range(16):
                fns.append(mm(T[bank][0:8, k:512:16], T.idp[:, 8 * k:8 * k + 8], T[buf][:, 32 * b:32 * b + 32],
                              j == 0 and k == 0, j == 1 and k == 15))
        emit("P", fns, [X("idp", 0, 128), X("fh", 0, 128), X("fl", 0, 128)], [X(bank, 0, 512)])
        emit("A", [lambda: g.scalar.activation(T.OK[0:8, 512 * b:512 * b + 512], T[bank][0:8, 0:512], AF.Copy)],
             [X(bank, 0, 512)], [o])
        dma("S", T.yk[:, 512 * b:512 * b + 512], T.OK[0:8, 512 * b:512 * b + 512], [o], [])
    cnt["sent"] = nsent[0]
    for s, c in cnt.items():
        g.wait_ge(T.sem[s], c)
